import numpy as np, ml_dtypes
CORES = [10,34,74,98]
N = 4
import mx_ref
BF = ml_dtypes.bfloat16
def cols(t, e):
    v = np.concatenate([t.reshape(128, -1, 4), np.zeros((128, 1, 4), BF)], axis=1)
    return np.ascontiguousarray(v[:, e]).reshape(128, -1)
def cut(t, i, w=512):
    return t[:, w * i:w * i + w]
def pick(q, e):
    c = np.concatenate([q[0].reshape(128, -1, 4), np.zeros((128, 1, 4), np.uint8)], axis=1); s = np.concatenate([q[1], np.ones((16, 1), np.uint8)], axis=1)
    return (np.ascontiguousarray(c[:, e].reshape(128, -1)), np.ascontiguousarray(s[:, e]))
def join(*qs):
    return (np.concatenate([q[0] for q in qs], axis=1), np.concatenate([q[1] for q in qs], axis=1))
def put(q, e, v):
    c, s = q[0].reshape(128, -1, 4).copy(), q[1].copy(); c[:, e] = v[0].reshape(128, -1, 4); s[:, e] = v[1]
    return (c.reshape(128, -1), s)
def pk(c, s):
    return (np.ascontiguousarray(c), mx_ref.live(s))
def emit(q):
    return q[0], q[1]
def decode(q):
    o = []
    for b in range(4):
        e = np.zeros((128, 128, 4), np.float32); e[np.arange(128), np.arange(128), b] = 1
        o.append(mx_ref.matmul(mx_ref.quantize(e.reshape(128, 512).astype(BF)), q))
    return np.stack(o, axis=2).reshape(128, -1)
def f(rng, *shape):
    return mx_ref.flush((rng.standard_normal(shape, dtype=np.float32) * np.exp2(rng.integers(-2, 3, shape[:-1] + (1,)))).astype(BF))
def wide(rng, *shape, cols=0):
    v = rng.standard_normal(shape, dtype=np.float32) * np.exp2(rng.integers(-12, 13, shape)).astype(np.float32)
    if cols: v *= np.repeat(np.exp2(rng.integers(-cols, cols + 1, shape[:-2] + (1, shape[-1] // 4))) * (rng.random(shape[:-2] + (1, shape[-1] // 4)) > 0.0625), 4, axis=-1).astype(np.float32)
    return mx_ref.flush(v.astype(BF))
M, A, E, R, O = 384, 32, 40, 3, 1
def big(v):
    v = v.astype(np.float32)
    v[np.abs(v) < np.float32(2.0 ** -14)] = 0
    return v.astype(BF)
def plain(rng):
    return {"me": big(f(rng, N, 128, 4 * M)), "x": big(f(rng, N, 128, 4 * A)), "w": f(rng, N, 128, 512 * O)}
def signs(rng, n):
    h = np.ones((1, 1))
    while len(h) < n: h = np.block([[h, h], [h, -h]])
    return h[rng.permutation(n)[:128]][:, rng.permutation(n)] * rng.choice([-1.0, 1.0], n)
def tiles(v):
    return v.reshape(-1, 128, 4).transpose(1, 0, 2).reshape(128, -1)
def store(rng, m, q):
    return {"me": big(np.stack([tiles(v) for v in m.reshape(N, M, 512)])), "x": big(np.stack([tiles(v) for v in q.reshape(N, A, 512)])), "w": f(rng, N, 128, 512 * O)}
def low(rng):
    return rng.standard_normal((N * M, 512), dtype=np.float32) * np.float32(2.0 ** -6)
def rough(rng, v):
    return v * (1 + 0.0625 * rng.uniform(-1, 1, v.shape)) * np.exp2(rng.integers(0, 2, (len(v), 1)))
def places(rng, s):
    at = np.zeros(len(s), int)
    for r in range(N):
        j = np.flatnonzero(s == r)
        at[j] = r * M + rng.permutation(M)[:len(j)]
    return at
def spare(rng, r, at):
    return rng.permutation(np.setdiff1d(np.arange(r * M, r * M + M), at))
def planted(rng, at, o):
    k, i = np.unique(at, return_inverse=True)
    v, m = signs(rng, 512), low(rng)
    m[k] = rough(rng, v[:len(k)])
    m[at[o[0]]] *= 8
    q = rough(rng, v[i])
    q[o[0]] = 4 * v[i[o[0]]] + 8 * v[i[o[-1]]]
    q[o[2]] = q[o[1]]
    return store(rng, m, q)
def setup_inputs(rng):
    return plain(rng)
def setup_inputs_hot(rng):
    h = int(rng.integers(0, N))
    g = (h + int(rng.integers(1, N))) % N
    at = (h + rng.integers(1, N, 128)) % N * M + rng.integers(0, M, 128)
    o = np.flatnonzero(np.arange(128) // A != h)
    p, u = h * M + rng.permutation(M)[:7], g * M + rng.permutation(M)[:6]
    at[o] = u[rng.integers(0, 6, len(o))]
    k = np.concatenate([o[:A], rng.permutation(o[A:-1])[:len(o) // 2 - A - 1]])
    at[k] = p[rng.integers(0, 6, len(k))]
    at[o[2]] = at[o[1]]
    at[o[-1]] = p[6]
    return planted(rng, at, o)
def setup_inputs_ties(rng):
    d, b = plain(rng), int(rng.integers(2, N))
    g = np.full((N, 4), 4.0)
    g[b] = 1
    g[(b + int(rng.integers(1, N))) % N] = 16
    p = big(np.abs(f(rng, 128, 16 * N).astype(np.float32)) * np.repeat(g.reshape(-1), 4))
    k = f(rng, 128, 120).astype(np.float32)
    k[:, :96] = np.abs(k[:, :96])
    k[:, :48] = -k[:, :48]
    k[:, :16] = k[:, :16] * np.float32(2.0 ** 24)
    k = big(k)
    e = rng.permutation(np.concatenate([np.arange(30), rng.integers(12, 24, 58), rng.integers(0, 30, 40)]))
    m = []
    for r in range(N):
        own = np.concatenate([4 * r + np.arange(4), 4 * ((r + 1) % N) + np.arange(4)])
        m.append(cols(p, rng.permutation(np.concatenate([own, own, own[rng.integers(0, 8, M - 16)]]))))
    d["me"] = np.stack(m)
    d["x"] = np.stack([cols(k, e[r * A:r * A + A]) for r in range(N)])
    return d
def setup_inputs_second(rng):
    a, b = signs(rng, 256), signs(rng, 256)
    s = rng.permutation(np.arange(128) % N)
    p = places(rng, np.concatenate([s, (s + rng.integers(1, N, 128)) % N]))
    e = rng.permutation(512)
    e, g = e[:256], e[256:]
    m, q = low(rng), rng.uniform(-1, 1, (128, 512)) * 2.0 ** -6
    q[:, e] = a
    m[p[:128, None], e] = a
    m[p[:128, None], g] = 4 * b
    m[p[128:, None], g] = 16 * b
    return store(rng, m, q)
def setup_inputs_idle(rng):
    o = rng.permutation(N)
    s = o[rng.integers(2, N, 128)]
    s[rng.permutation(128)[:E]] = o[1]
    at = places(rng, s)
    j = int(np.argmin(s))
    z = np.sort(spare(rng, int(s[j]), at)[:2])
    at[j] = z[0]
    far = spare(rng, int(s.max()), at)[0]
    v, m = signs(rng, 512), low(rng)
    v = v * v[j]
    m[at] = rough(rng, v)
    m = m - np.float32(0.25)
    m[[z[0], z[1], far]] = 0
    q = rough(rng, v)
    q[j] = 2 * q[j]
    d = store(rng, m * np.float32(2.0 ** 27), q * 2.0 ** 27)
    c = 4 * int(z[0] % M)
    d["me"][int(s[j]), :, c:c + 4] = BF(-0.0)
    return d
def setup_inputs_spread(rng):
    return {**plain(rng), "me": big(wide(rng, N, 128, 4 * M, cols=3)), "x": big(wide(rng, N, 128, 4 * A, cols=3))}
def check_inputs(d):
    b = []
    for k, least in (("me", 2.0 ** -14), ("x", 2.0 ** -14), ("w", 2.0 ** -30)):
        v = np.abs(d[k].astype(np.float32))
        if not (np.isfinite(v).all() and ((v == 0) | (v >= least) & (v <= 2.0 ** 30)).all()): b.append("a value of " + k)
    return b
def reference(me, x, w):
    mem = [mx_ref.quantize(np.ascontiguousarray(me[r])) for r in range(N)]
    q = join(*[mx_ref.quantize(np.ascontiguousarray(x[r])) for r in range(N)])
    wi = np.zeros((N, R, 128), np.float32)
    for t in range(R):
        s = np.concatenate([mx_ref.matmul(q, mem[r]) for r in range(N)], axis=1) + np.float32(0)
        win = np.argmax(s, axis=1)
        answered = np.zeros(128, bool)
        for r in range(N): answered[np.flatnonzero(win // M == r)[:E]] = True
        wi[:, t] = np.where(answered, win, -1 - win)
        half = decode(pick(join(*mem), win)) * np.float32(0.5)
        new = mx_ref.quantize((half + decode(q) * np.float32(0.5)).astype(BF))
        a = np.flatnonzero(answered)
        q = put(q, a, pick(new, a))
        for r in range(N):
            j = a[win[a] // M == r]
            if j.size:
                c, i = np.unique(win[j] - r * M, return_index=True)
                mem[r] = put(mem[r], c, pick(new, j[i]))
    oc, osc, y = np.zeros((N, 128, 4 * M), np.uint8), np.zeros((N, 16, M), np.uint8), np.zeros((N, 128, 128 * O), np.float32)
    for r in range(N):
        oc[r], osc[r] = emit(mem[r])
        for o in range(O): y[r, :, 128 * o:128 * o + 128] = mx_ref.matmul(mx_ref.quantize(np.ascontiguousarray(cut(w[r], o))), q)
    return {"oc": oc, "osc": osc, "wi": wi, "y": y}

@@ -1,0 +1,392 @@
+from concourse.bass import DstId, RemoteDMATransfer
+from concourse.mybir import dt, AluOpType, ActivationFunctionType, AxisListType
+
+M, A, E, R = 384, 32, 40, 3
+HM = M // 2
+SL = 48
+QW, QL = 128 + 4 * SL, 128 + 4 * 128
+FW = 14000
+CODE, U8, F32, BF, I32, U16 = "float8_e4m3fn_x4", "uint8", "float32", "bfloat16", "int32", "uint16"
+
+SCRATCH = {
+    "xt": ("sbuf", [128, 512], BF), "xq": ("sbuf", [128, 128], CODE), "xs": ("sbuf", [128, 128], U8),
+    "met": ("sbuf", [128, 4 * M], BF),
+    "wt": ("sbuf", [128, 512], BF), "wq": ("sbuf", [128, 128], CODE), "ws": ("sbuf", [128, 128], U8),
+    "ce": ("sbuf", [128, 520 + 1024], F32), "et": ("sbuf", [128, 2048], BF), "eq": ("sbuf", [128, 512], CODE), "es": ("sbuf", [128, 512], U8),
+    "ints": ("sbuf", [128, 64], I32),
+    "cf": ("sbuf", [128, 1100], F32),
+    "ff": ("sbuf", [128, FW], F32),
+    "offx": ("sbuf", [128, 2], U16),
+    "places": ("sbuf", [128, 4], F32), "landp": ("sbuf", [128, 12], F32),
+    "yo": ("sbuf", [128, 128], F32),
+    "m3": ("sbuf", [128, M], CODE), "ms3": ("sbuf", [128, M], U8),
+    "q3": ("sbuf", [128, 128], CODE), "qs3": ("sbuf", [128, 128], U8),
+    "pscore": ("psum", [128, 1024], F32), "pblend": ("psum", [128, 2048], F32), "py": ("psum", [128, 512], F32),
+}
+SEMAPHORES = ["cv", "cs", "ct", "cg", "lx", "lm", "lw", "x0", "xp", "loc", "out"]
+for _t in range(R):
+    _w = QL if _t == R - 1 else QW
+    SCRATCH.update({
+        "m%d" % _t: ("sbuf", [128, 128 + M], CODE), "ms%d" % _t: ("sbuf", [128, 128 + M], U8),
+        "q%d" % _t: ("sbuf", [128, _w], CODE), "qs%d" % _t: ("sbuf", [128, _w], U8),
+        "p%d" % _t: ("sbuf", [128, 128], CODE), "ps%d" % _t: ("sbuf", [128, 128], U8),
+        "s%d" % _t: ("sbuf", [128, SL], CODE), "ss%d" % _t: ("sbuf", [128, SL], U8),
+        "h%d" % _t: ("sbuf", [128, 512], BF),
+        "land%d" % _t: ("sbuf", [128, 8], F32),
+        "oc%d" % _t: ("sbuf", [128, 8], U16), "og%d" % _t: ("sbuf", [128, 4], U16),
+        "oq%d" % _t: ("sbuf", [128, 8], U16), "om%d" % _t: ("sbuf", [128, 24], U16),
+    })
+    SEMAPHORES += ["x1_%d" % _t, "x2_%d" % _t, "own%d" % _t]
+
+
+def rank_program(g, core, T, topo):
+    r = T.rank_of(core)
+    if r is None:
+        return
+    AF, OP, AXIS = ActivationFunctionType, AluOpType, AxisListType.X
+    V, S, TE = g.vector, g.scalar, g.tensor
+    others = [(r + k) % 4 for k in (1, 2, 3)]
+    queue = {"v": V, "s": S, "t": TE, "g": g, "y": g.sync}
+    count = {"v": 0, "s": 0, "t": 0, "g": 0}
+    seen = {k: {} for k in queue}
+    sem = T.sem
+
+    def need(q, *deps):
+        want = {}
+        for d in deps:
+            if d is not None:
+                want[d[0]] = max(want.get(d[0], 0), d[1])
+        for n, v in want.items():
+            if seen[q].get(n, 0) < v:
+                queue[q].wait_ge(sem[n], v)
+                seen[q][n] = v
+
+    def did(q, ins):
+        count[q] += 1
+        ins.then_inc(sem["c" + q], 1)
+        return ("c" + q, count[q])
+
+    def ts(out, in0, s1, op0, s2=None, op1=None, deps=()):
+        need("v", *deps)
+        if op1 is None:
+            return did("v", V.tensor_scalar(out, in0, s1, None, op0))
+        return did("v", V.tensor_scalar(out, in0, s1, s2, op0, op1))
+
+    def tt(out, a, b, op, deps=()):
+        need("v", *deps)
+        return did("v", V.tensor_tensor(out, a, b, op))
+
+    def red(out, a, op, deps=()):
+        need("v", *deps)
+        return did("v", V.tensor_reduce(out, a, AXIS, op))
+
+    def scan(out, a, b, op0, op1, init, deps=()):
+        need("v", *deps)
+        return did("v", V.tensor_tensor_scan(out, a, b, init, op0, op1))
+
+    def tr(out, a, deps=()):
+        need("v", *deps)
+        return did("v", V.transpose(out, a))
+
+    def cp(out, a, deps=()):
+        need("v", *deps)
+        return did("v", V.tensor_copy(out, a))
+
+    def fill(ap, c):
+        return did("v", V.memset(ap, c))
+
+    def qmx(o, s, i, deps=()):
+        need("v", *deps)
+        return did("v", V.quantize_mx(o, s, i))
+
+    def act(out, a, func, deps=(), **k):
+        need("s", *deps)
+        return did("s", S.activation(out, a, func, **k))
+
+    def mm(out, l, ls, x, xs, start, stop, deps=()):
+        need("t", *deps)
+        return did("t", TE.matmul_mx(out, l, ls, x, xs, start, stop))
+
+    def io(*a, **k):
+        return did("g", g.iota(*a, **k))
+
+    used, cpos = [0], [0]
+
+    def new(n):
+        o = used[0]
+        used[0] = o + (n + 7) // 8 * 8
+        assert used[0] <= FW
+        return o
+
+    def F(o, c0, c1, p0=0, p1=128, st=1):
+        return T.ff[p0:p1, o + c0:o + c1:st]
+
+    def cnew(n):
+        o = cpos[0]
+        cpos[0] = o + (n + 7) // 8 * 8
+        return o
+
+    def C(o, c0, c1, p0=0, p1=128, st=1):
+        return T.cf[p0:p1, o + c0:o + c1:st]
+
+    local = [0]
+
+    def send(src, dsts, rsem, deps):
+        need("g", *deps)
+        mask = topo.mask(core, T.cores[others[0]])
+        ids = []
+        for s in others:
+            rid, pid, _ = topo.addr(T.cores[s])
+            mask &= topo.mask(core, T.cores[s])
+            ids.append(DstId(rid=rid, pnc=pid))
+        g.remote_dma_fused([RemoteDMATransfer(dst_ids=ids, dma_engine_mask=mask, remote_sem=sem[rsem], srcs=[src], dsts=dsts)],
+                           local_sem=sem["loc"])
+        local[0] += bin(mask).count("1")
+
+    u8, u32 = dt.uint8, dt.uint32
+    ne = len(topo.engines(core, T.cores[others[0]]))
+
+    g.sync.dma_start(T.xt[:, 0:4 * A], T.x[:, :]).then_inc(sem.lx, 16)
+    S.dma_start(T.met[:, 0:2 * M], T.me[:, 0:2 * M]).then_inc(sem.lm, 16)
+    g.sync.dma_start(T.met[:, 2 * M:4 * M], T.me[:, 2 * M:4 * M]).then_inc(sem.lm, 16)
+    g.sync.dma_start(T.wt[:, :], T.w[:, :]).then_inc(sem.lw, 16)
+
+    small = {"allow_small_or_imprecise_dtypes": True}
+    cRow, cFour = cnew(32), cnew(4)
+    cNeg, cKeep, cE, cZero, c2k = cnew(HM), cnew(128), cnew(128), cnew(32), cnew(32)
+    cJ, cM16, cKb, cKc, cT0, cT1, cPl, cNp, cP31, cB = [cnew(n) for n in (1, 1, 3, 1, 1, 1, 3, 3, 1, 1)]
+    cMask, cTri, cNm = cnew(32), cnew(32), cnew(32)
+    i0 = io(T.ints[:, 0:1], [[0, 1]], 0, 1)
+    i5 = io(T.ce[:, 0:512], [[1, 512]], 0, 0, **small)
+    i4 = io(T.ce[:, 512:516], [[1, 4]], 0, 4, **small)
+    z0 = fill(T.xt[:, 4 * A:512], 0.0)
+    b0 = ts(T.ints[:, 1:2], T.ints[:, 0:1], 15, OP.bitwise_and, deps=[i0])
+    a0 = cp(C(cJ, 0, 1), T.ints[:, 0:1])
+    b1 = ts(T.ints[:, 2:3], T.ints[:, 0:1], 31, OP.bitwise_and)
+    b2 = ts(T.ints[:, 3:4], T.ints[:, 0:1], 5, OP.arith_shift_right)
+    a1 = cp(C(cM16, 0, 1), T.ints[:, 1:2], [b0])
+    for c in range(3):
+        kKb = ts(C(cKb, c, c + 1), C(cM16, 0, 1), 16.0 * c + 0.5, OP.add, deps=[a1])
+    kOx = ts(T.offx[:, 0:2], C(cKb, 0, 2), -0.5, OP.add, deps=[kKb])
+    qx = qmx(T.xq[:, :], T.xs[:, :], T.xt[:, :], [("lx", 16), z0])
+    o0, o1 = A * r, A * r + A
+    send(T.xq[:, 0:A].bitcast(u8), [T.q0[:, o0:o1].bitcast(u8)] * 3, "x0", [qx])
+    send(T.xs[:, 0:A], [T.qs0[:, o0:o1]] * 3, "x0", [qx])
+    i1 = io(T.ints[:, 16:48], [[1, 32]], 128, -1)
+    i2 = io(C(cRow, 0, 32), [[1, 32]], 0, 0, **small)
+    i3 = io(C(cFour, 0, 4), [[1, 4]], 1, 0, **small)
+    own = cp(T.q0[:, o0:o1].bitcast(u32), T.xq[:, :].bitcast(u32).indirect(T.offx[:, 0:2]), [kOx, qx])
+    owns = act(T.qs0[:, o0:o1], T.xs[:, :].indirect(T.offx[:, 0:2]), AF.Copy, [kOx, qx])
+    ke = []
+    for b in range(2):
+        x = act(T.ce[:, 520 + 512 * b:1032 + 512 * b], T.ce[:, 0:512], AF.Abs, [i4, i5], scale=-1.0, bias=T.ce[:, 512 + b:513 + b])
+        ke.append(act(T.et[:, 512 * b:512 * b + 512], T.ce[:, 520 + 512 * b:1032 + 512 * b], AF.Relu, [x], scale=-1.0, bias=0.5))
+    a2 = cp(C(cP31, 0, 1), T.ints[:, 2:3], [b1])
+    a3_ = ts(C(cB, 0, 1), T.ints[:, 3:4], 64.0, OP.mult, deps=[b2])
+    f0 = fill(C(cNeg, 0, HM), -1e29)
+    f1 = fill(C(cKeep, 0, 128), 1.0)
+    f2 = fill(C(cE, 0, 128), float(E))
+    f3 = fill(C(cZero, 0, 32), 0.0)
+    memd = qmx(T.m0[:, 128:128 + M], T.ms0[:, 128:128 + M], T.met[:, :], [("lm", 32)])
+    for b in (2, 3):
+        ke.append(ts(T.et[:, 512 * b:512 * b + 512], T.ce[:, 0:512], T.ce[:, 512 + b:513 + b], OP.is_equal, 0.5, OP.mult, deps=[i4, i5]))
+    f4 = fill(C(c2k, 0, 32), 2048.0)
+    need("v", f1)
+    f1 = fill(C(cKeep, 0, 128, st=16), 0.0)
+    b3 = ts(T.ints[:, 16:48], T.ints[:, 16:48], 15, OP.bitwise_and, deps=[i1])
+    kKc = ts(C(cKc, 0, 1), C(cJ, 0, 1), 2048.0, OP.add, deps=[a0])
+    kT = ts(C(cT0, 0, 1), C(cJ, 0, 1), -1.0, OP.mult, float(127 - SL), OP.add)
+    kT = ts(C(cT1, 0, 1), C(cJ, 0, 1), -1.0, OP.mult, float(127 - SL + E), OP.add)
+    kmask = ts(C(cMask, 0, 32), T.ints[:, 16:48], 0.0, OP.is_equal, 1e6, OP.mult, deps=[b3])
+    for h in range(3):
+        kPl = ts(C(cPl, h, h + 1), C(cB, 0, 1), C(cJ, 0, 1), OP.add, 128.0 + 32 * h, OP.add, deps=[a3_])
+    kTri = ts(C(cTri, 0, 32), C(cRow, 0, 32), C(cP31, 0, 1), OP.is_ge, 1e6, OP.mult, deps=[a2, i2])
+    kNm = ts(C(cNm, 0, 32), C(cMask, 0, 32), float(HM) - 1e6, OP.add, deps=[kmask])
+    kNp = ts(C(cNp, 0, 3), C(cPl, 0, 3), -127.0, OP.add, -2048.0, OP.mult, deps=[kPl])
+    ke = qmx(T.eq[:, :], T.es[:, :], T.et[:, :], ke)
+    WR, OH, A3, KF, K2, RW3 = new(128), new(12), new(3), new(136), new(136), new(16 * R)
+    fWR = fill(F(WR, 0, 128), 0.0)
+    fKF = fill(F(KF, 128, 136), 0.0)
+    fK2 = fill(F(K2, 128, 136), -128.0)
+    fRW = fill(F(RW3, 0, 16 * R), -1e29)
+    kw = qmx(T.wq[:, :], T.ws[:, :], T.wt[:, :], [("lw", 16)])
+
+    qdeps = [own, owns, ("x0", 2 * ne * 3)]
+    mdeps = [memd]
+    scan_prev, cast_prev = [None, None], []
+    for t in range(R):
+        land = T["land%d" % t]
+        m, ms, q, qs = T["m%d" % t], T["ms%d" % t], T["q%d" % t], T["qs%d" % t]
+        p, ps, s_, ss_ = T["p%d" % t], T["ps%d" % t], T["s%d" % t], T["ss%d" % t]
+        h = T["h%d" % t]
+        oc, og, oq, om = T["oc%d" % t], T["og%d" % t], T["oq%d" % t], T["om%d" % t]
+        last = t == R - 1
+        x1, x2 = "x1_%d" % t, "x2_%d" % t
+        RM, JK, CN, C0, C1 = new(M), new(M), new(1), new(1), new(1)
+        half = [F(RM, k, M, st=2) for k in range(2)]
+        top = [F(RM, M - 2 + k, M - 1 + k) for k in range(2)]
+        rm = []
+        for k in range(2):
+            rm.append(mm(T.pscore[:, 512 * k:512 * k + HM], q[:, 0:128], qs[:, 0:128], m[:, 128 + HM * k:128 + HM * k + HM],
+                         ms[:, 128 + HM * k:128 + HM * k + HM], True, True, qdeps + mdeps + [scan_prev[k]]))
+        rm = [scan(half[k], T.pscore[:, 512 * k:512 * k + HM], C(cNeg, 0, HM), OP.max, OP.max, -1e29, [rm[k], f0]) for k in range(2)]
+        scan_prev = rm
+        send(F(RM, M - 2, M), [land[:, 2 * r:2 * r + 2]] * 3, x1, rm)
+        for b in range(4):
+            dq = mm(T.pblend[:, 512 * b:512 * b + 128], T.eq[:, 128 * b:128 * b + 128], T.es[:, 128 * b:128 * b + 128],
+                    q[:, 0:128], qs[:, 0:128], True, False, [ke] + cast_prev)
+        B1, R1, R2, FC, K1, BA, NM, ME = new(32), new(128), new(128), new(1), new(1), new(1), new(32), new(1)
+        c0_ = act(F(JK, 0, HM), half[0], AF.Sign, [rm[0]], scale=-1.0, bias=top[0], accum_out=F(C0, 0, 1))
+        c1_ = act(F(JK, HM, M), half[1], AF.Sign, [rm[1]], scale=-1.0, bias=top[1], accum_out=F(C1, 0, 1))
+        k1 = ts(F(K1, 0, 1), top[1], top[0], OP.is_le, 1e5, OP.mult, deps=rm)
+        fc = ts(F(FC, 0, 1), top[1], top[0], OP.is_gt, 1e5, OP.mult)
+        mx = tt(F(ME, 0, 1), top[0], top[1], OP.max)
+        nm = ts(F(NM, 0, 32), C(cNm, 0, 32), F(K1, 0, 1), OP.add, deps=[k1, kNm])
+        ba = ts(F(BA, 0, 1), F(FC, 0, 1), F(C0, 0, 1), OP.add, deps=[fc, c0_])
+        bc = ts(F(B1, 0, 32), F(NM, 0, 32), F(C1, 0, 1), OP.add, F(BA, 0, 1), OP.min, deps=[nm, ba, c1_])
+        for a in range(4):
+            x = tr(F(R1, 32 * a, 32 * a + 32, 0, 32), F(B1, 0, 32, 32 * a, 32 * a + 32), [bc])
+        k1 = ts(F(K1, 0, 1), F(K1, 0, 1), float(HM), OP.add)
+        x = scan(F(R2, 0, 128, 0, 32), C(cKeep, 0, 128, 0, 32), F(R1, 0, 128, 0, 32), OP.mult, OP.max, 0.0, [x, f1])
+        cn = ts(F(CN, 0, 1), F(C1, 0, 1), F(K1, 0, 1), OP.add, F(BA, 0, 1), OP.min, deps=[k1])
+        for a in range(4):
+            lc = cp(oc[32 * a:32 * a + 32, 0:8], F(R2, 15, 128, 0, 32, 16), [x])
+        OW, KB = new(32), new(32)
+        ow = act(F(OW, 0, 32), C(cZero, 0, 32), AF.Identity, [f3, mx], bias=F(ME, 0, 1))
+        kb = act(F(KB, 0, 32), C(c2k, 0, 32), AF.Identity, [f4, cn, kKc], scale=F(CN, 0, 1), bias=C(cKc, 0, 1))
+        pl = act(T.places[:, t:t + 1], F(CN, 0, 1), AF.Copy, [cn], bias=float(M * r))
+        if last:
+            send(T.places[:, 0:R], [T.landp[:, R * r:R * r + R]] * 3, "xp", [pl])
+        pkc = cp(p[:, :].bitcast(u32), m[:, 128:128 + M].bitcast(u32).indirect(oc[:, 0:8]), [lc] + mdeps)
+        pks = act(ps[:, :], ms[:, 128:128 + M].indirect(oc[:, 0:8]), AF.Copy, [lc] + mdeps)
+        for a in range(4):
+            kf = tr(F(KF, 32 * a, 32 * a + 32, 0, 32), F(KB, 0, 32, 32 * a, 32 * a + 32), [kb])
+        bl = []
+        for b in range(4):
+            bl.append(mm(T.pblend[:, 512 * b:512 * b + 128], T.eq[:, 128 * b:128 * b + 128], T.es[:, 128 * b:128 * b + 128],
+                         p[:, :], ps[:, :], False, True, [pkc, pks]))
+        cast_prev = []
+        for b in (0, 2):
+            cast_prev.append(act(h[:, b:512:4], T.pblend[:, 512 * b:512 * b + 128], AF.Copy, [bl[b]]))
+            cast_prev.append(cp(h[:, b + 1:512:4], T.pblend[:, 512 * b + 512:512 * b + 640], [bl[b + 1]]))
+        for b in (1, 2, 3):
+            kk = act(F(KF, 0, 128, 32 * b, 32 * b + 32), F(KF, 0, 128, 0, 32), AF.Copy, [kf])
+        nd = qmx(m[:, 0:128], ms[:, 0:128], h[:, :], cast_prev)
+        if last:
+            k0 = 128 + 128 * r
+            send(m[:, 0:128].bitcast(u8), [q[:, k0:k0 + 128].bitcast(u8)] * 3, x2, [nd])
+            send(ms[:, 0:128], [qs[:, k0:k0 + 128]] * 3, x2, [nd])
+            need("y", nd)
+            g.sync.dma_start(q[:, k0:k0 + 128].bitcast(u8), m[:, 0:128].bitcast(u8)).then_inc(sem["own%d" % t], 16)
+            g.sync.dma_start(qs[:, k0:k0 + 128], ms[:, 0:128]).then_inc(sem["own%d" % t], 16)
+        x1 = (x1, 3 * ne)
+        MX, FL, MI, MR, AC, CS = new(1), new(1), new(32), new(128), new(3), new(128)
+        RW, S1, J3, BW, BT = RW3 + 16 * t, new(1), new(5), new(32), new(32)
+        lo = act(land[:, 2 * r:2 * r + 2], F(RM, M - 2, M), AF.Copy, [x1])
+        if r == 0:
+            x = red(F(MX, 0, 1), land[:, 2:8], OP.max, [x1])
+            mi = ts(F(MI, 0, 32), F(OW, 0, 32), F(MX, 0, 1), OP.is_ge, deps=[x, ow])
+        elif r == 3:
+            x = red(F(MX, 0, 1), land[:, 0:6], OP.max, [x1])
+            mi = ts(F(MI, 0, 32), F(OW, 0, 32), F(MX, 0, 1), OP.is_gt, deps=[x, ow])
+        elif r == 1:
+            x = red(F(MX, 0, 1), land[:, 4:8], OP.max, [x1])
+            x = ts(F(FL, 0, 1), land[:, 0:1], land[:, 1:2], OP.max, F(ME, 0, 1), OP.is_lt, deps=[mx])
+            mi = ts(F(MI, 0, 32), F(OW, 0, 32), F(MX, 0, 1), OP.is_ge, F(FL, 0, 1), OP.mult, deps=[x, ow])
+        else:
+            x = red(F(MX, 0, 1), land[:, 0:4], OP.max, [x1])
+            x = ts(F(FL, 0, 1), land[:, 6:7], land[:, 7:8], OP.max, F(ME, 0, 1), OP.is_le, deps=[mx])
+            mi = ts(F(MI, 0, 32), F(OW, 0, 32), F(MX, 0, 1), OP.is_gt, F(FL, 0, 1), OP.mult, deps=[x, ow])
+        for a in range(4):
+            x = tr(F(MR, 32 * a, 32 * a + 32, 0, 32), F(MI, 0, 32, 32 * a, 32 * a + 32), [mi])
+        cs = scan(F(CS, 0, 128, 0, 32), F(MR, 0, 128, 0, 32), C(cE, 0, 128, 0, 32), OP.add, OP.min, 0.0, [x, f2])
+        for c in range(2):
+            ac = act(F(new(128), 0, 128, 0, 32), F(CS, 0, 128, 0, 32), AF.Sign, [cs, kKb], scale=-1.0, bias=C(cKb, c, c + 1, 0, 32),
+                     accum_out=F(AC, c, c + 1, 0, 32))
+        x = ts(F(K2, 0, 128, 0, 32), F(CS, 0, 128, 0, 32), C(cKb, 2, 3, 0, 32), OP.is_le, 2.0, OP.mult, deps=[cs, kKb])
+        rw = scan(F(RW, 1, 9), land[:, 0:8], C(cNeg, 0, 8), OP.max, OP.max, -1e29, [lo, x1, fRW])
+        av = red(F(AC, 2, 3, 0, 32), F(K2, 0, 129, 0, 32), OP.add, [x, fK2])
+        EQ, T1 = new(136), new(1)
+        s1 = act(F(J3, 0, 5), F(RW, 0, 9, st=2), AF.Sign, [rw], scale=-1.0, bias=F(RW, 8, 9), accum_out=F(S1, 0, 1))
+        bw = act(F(BW, 0, 32), C(cZero, 0, 32), AF.Identity, [s1], bias=F(S1, 0, 1))
+        for a in range(4):
+            lg = ts(og[32 * a:32 * a + 32, 0:3], F(AC, 0, 3, 0, 32), 0.5, OP.mult, 64.0, OP.add, deps=[ac, av])
+        if not last:
+            gc = cp(s_[:, :].bitcast(u32), m[:, :].bitcast(u32).indirect(og[:, 0:3]), [lg, nd])
+            gs = act(ss_[:, :], ms[:, :].indirect(og[:, 0:3]), AF.Copy, [lg, nd])
+            k0 = 128 + SL * r
+            send(s_[:, 0:E].bitcast(u8), [q[:, k0:k0 + E].bitcast(u8)] * 3, x2, [gc])
+            send(ss_[:, 0:E], [qs[:, k0:k0 + E]] * 3, x2, [gs])
+            need("y", gc, gs)
+            g.sync.dma_start(q[:, k0:k0 + SL].bitcast(u8), s_[:, :].bitcast(u8)).then_inc(sem["own%d" % t], 16)
+            g.sync.dma_start(qs[:, k0:k0 + SL], ss_[:, :]).then_inc(sem["own%d" % t], 16)
+        KG, AB, P, L, B2, R3, R4 = new(SL), new(3 * SL), new(1), new(1), new(32), new(128), new(128)
+        D, BM, R5, R6, LM, PS = new(3), new(96), new(96), new(96), new(24), new(1)
+        kg = act(F(KG, 0, SL), F(KF, 0, 136).indirect(og[:, 0:3]), AF.Copy, [kk, fKF, lg])
+        ab = [act(F(AB, SL * c, SL * c + SL), F(KG, 0, SL), AF.Abs, [kg, kNp], bias=C(cNp, c, c + 1)) for c in range(3)]
+        tc = act(F(EQ, 128, 129), F(S1, 0, 1), AF.Identity, [kT, s1], scale=float(SL), bias=C(cT0, 0, 1))
+        tc = act(F(T1, 0, 1), F(S1, 0, 1), AF.Identity, scale=float(SL), bias=C(cT1, 0, 1))
+        if last:
+            tc = act(F(PS, 0, 1), F(S1, 0, 1), AF.Copy, scale=128.0)
+        bt = ts(F(BT, 0, 32), C(cTri, 0, 32), F(S1, 0, 1), OP.min, deps=[s1, kTri])
+        for b in range(1, 4):
+            for a in range(b):
+                x = tr(F(WR, 32 + 32 * a, 64 + 32 * a, 32 * b, 32 * b + 32), F(BW, 0, 32, 32 * a, 32 * a + 32), [bw, fWR])
+        x = tr(F(WR, 0, 32), F(BT, 0, 32), [bt])
+        d = [red(F(D, c, c + 1), F(AB, SL * c, SL * c + SL), OP.min, [ab[c]]) for c in range(3)]
+        eq = ts(F(EQ, 0, 128), F(WR, 0, 128), F(S1, 0, 1), OP.is_equal, deps=[x])
+        pz = act(F(new(136), 0, 129), F(EQ, 0, 129), AF.Copy, [eq, tc], accum_out=F(P, 0, 1))
+        for c in range(3):
+            bm = ts(F(BM, 32 * c, 32 * c + 32), C(cMask, 0, 32), F(D, c, c + 1), OP.min, C(cPl, c, c + 1), OP.min, deps=[d[c]])
+        oh = ts(F(OH, t, 12, st=3), C(cFour, 0, 4), F(S1, 0, 1), OP.is_equal, deps=[i3])
+        y = tr(F(R5, 0, 96), F(BM, 0, 96), [bm])
+        z = ts(F(A3, t, t + 1), F(P, 0, 1), F(T1, 0, 1), OP.is_le, deps=[pz, tc])
+        y = scan(F(R6, 0, 96), C(cKeep, 0, 96), F(R5, 0, 96), OP.mult, OP.add, 0.0, [y])
+        z = ts(F(L, 0, 1), F(PS if last else P, 0, 1), F(A3, t, t + 1), OP.mult, C(cJ, 0, 1), OP.add, deps=[z])
+        lms = [act(F(LM, 6 * a, 6 * a + 6, 0, 32), F(R6, 15, 96, 32 * a, 32 * a + 32, 16), AF.Copy, [y]) for a in (2, 3)]
+        for a in range(2):
+            lmv = cp(F(LM, 6 * a, 6 * a + 6, 0, 32), F(R6, 15, 96, 32 * a, 32 * a + 32, 16), [y])
+        z = ts(F(B2, 0, 32), C(cMask, 0, 32), F(L, 0, 1), OP.min, deps=[z])
+        if last:
+            SG, AM = new(3), new(3)
+            lp = act(T.landp[:, R * r:R * r + R], T.places[:, 0:R], AF.Copy, [("xp", 3 * ne), pl])
+            sg = act(F(SG, 0, 3), F(A3, 0, 3), AF.Copy, [z], scale=2.0, bias=-1.0)
+            sg = act(F(AM, 0, 3), F(A3, 0, 3), AF.Copy, scale=1.0, bias=-1.0)
+        for a in range(4):
+            x = tr(F(R3, 32 * a, 32 * a + 32, 0, 32), F(B2, 0, 32, 32 * a, 32 * a + 32), [z])
+        for b in range(4):
+            lm = cp(om[32 * b:32 * b + 32, :], F(LM, 0, 24, 0, 32), [lmv] + lms)
+        x = scan(F(R4, 0, 128, 0, 32), C(cKeep, 0, 128, 0, 32), F(R3, 0, 128, 0, 32), OP.mult, OP.add, 0.0, [x])
+        if not last:
+            m2, ms2, c0 = T["m%d" % (t + 1)], T["ms%d" % (t + 1)], 128
+        else:
+            m2, ms2, c0 = T.m3, T.ms3, 0
+        mp = act(ms2[:, c0:c0 + M], ms[:, :].indirect(om[:, 0:24]), AF.Copy, [lm, nd] + mdeps)
+        for b in range(4):
+            lq = cp(oq[32 * b:32 * b + 32, :], F(R4, 15, 128, 0, 32, 16), [x])
+        mc = cp(m2[:, c0:c0 + M].bitcast(u32), m[:, :].bitcast(u32).indirect(om[:, 0:24]), [lm, nd] + mdeps)
+        mdeps = [mc, mp]
+        if last:
+            need("y", mc, mp)
+            g.sync.dma_start(T.oc[:, :], T.m3[:, :].bitcast(u8)).then_inc(sem.out, 16)
+            for k in range(4):
+                g.sync.dma_start(T.osc[4 * k:4 * k + 4, :], T.ms3[32 * k:32 * k + 4, :]).then_inc(sem.out, 16)
+            G12, G3, W1, WO = new(12), new(3), new(3), new(3)
+            x = tt(F(G12, 0, 12), F(OH, 0, 12), T.landp[:, :], OP.mult, [oh, lp, ("xp", 3 * ne)])
+            for c in range(3):
+                w = red(F(G3, c, c + 1), F(G12, c, 12, st=3), OP.add, [x])
+        q2, qs2 = T["q%d" % (t + 1)], T["qs%d" % (t + 1)]
+        ready = [lq, (x2, 2 * 3 * ne), ("own%d" % t, 32)] + qdeps
+        qdeps = [cp(q2[:, 0:128].bitcast(u32), q[:, :].bitcast(u32).indirect(oq[:, 0:8]), ready),
+                 act(qs2[:, 0:128], qs[:, :].indirect(oq[:, 0:8]), AF.Copy, ready)]
+    y = mm(T.py[:, 0:128], T.wq[:, :], T.ws[:, :], T.q3[:, :], T.qs3[:, :], True, True, [kw] + qdeps)
+    x = tt(F(W1, 0, 3), F(G3, 0, 3), F(SG, 0, 3), OP.mult, [w, sg])
+    x = tt(F(WO, 0, 3), F(W1, 0, 3), F(AM, 0, 3), OP.add, [x])
+    y = act(T.yo[:, :], T.py[:, 0:128], AF.Copy, [y])
+    need("y", x)
+    for c in range(R):
+        g.sync.dma_start(T.wi[c:c + 1, :], F(WO, c, c + 1)).then_inc(sem.out, 16)
+    need("s", y)
+    S.dma_start(T.y[:, :], T.yo[:, :]).then_inc(sem.out, 16)
+    need("y", ("out", 16 * (1 + 4 + R + 1)))
+    need("g", ("loc", local[0]), *[("c" + k, n) for k, n in count.items()])

@@ -4,16 +4,18 @@ from concourse.mybir import dt, AluOpType, ActivationFunctionType, AxisListType
 M, A, E, R = 384, 32, 40, 3
 HM = M // 2
 SL = 48
-QW, QL = 128 + 4 * SL, 128 + 4 * 128
-FW = 14000
+SP = 128 + M
+QW, QL = 128 + 4 * SL, 128 + 4 * SP
+FW = 9000
+STEP = 4096.0
 CODE, U8, F32, BF, I32, U16 = "float8_e4m3fn_x4", "uint8", "float32", "bfloat16", "int32", "uint16"
 
 SCRATCH = {
     "xt": ("sbuf", [128, 512], BF), "xq": ("sbuf", [128, 128], CODE), "xs": ("sbuf", [128, 128], U8),
     "met": ("sbuf", [128, 4 * M], BF),
     "wt": ("sbuf", [128, 512], BF), "wq": ("sbuf", [128, 128], CODE), "ws": ("sbuf", [128, 128], U8),
-    "ce": ("sbuf", [128, 520 + 1024], F32), "et": ("sbuf", [128, 2048], BF), "eq": ("sbuf", [128, 512], CODE), "es": ("sbuf", [128, 512], U8),
-    "ints": ("sbuf", [128, 64], I32),
+    "et": ("sbuf", [128, 516], BF), "eq": ("sbuf", [128, 512], CODE), "es": ("sbuf", [128, 512], U8),
+    "ints": ("sbuf", [128, 136], I32),
     "cf": ("sbuf", [128, 1100], F32),
     "ff": ("sbuf", [128, FW], F32),
     "offx": ("sbuf", [128, 2], U16),
@@ -27,16 +29,16 @@ SEMAPHORES = ["cv", "cs", "ct", "cg", "lx", "lm", "lw", "x0", "xp", "loc", "out"
 for _t in range(R):
     _w = QL if _t == R - 1 else QW
     SCRATCH.update({
-        "m%d" % _t: ("sbuf", [128, 128 + M], CODE), "ms%d" % _t: ("sbuf", [128, 128 + M], U8),
         "q%d" % _t: ("sbuf", [128, _w], CODE), "qs%d" % _t: ("sbuf", [128, _w], U8),
         "p%d" % _t: ("sbuf", [128, 128], CODE), "ps%d" % _t: ("sbuf", [128, 128], U8),
-        "s%d" % _t: ("sbuf", [128, SL], CODE), "ss%d" % _t: ("sbuf", [128, SL], U8),
         "h%d" % _t: ("sbuf", [128, 512], BF),
-        "land%d" % _t: ("sbuf", [128, 8], F32),
+        "land%d" % _t: ("sbuf", [128, 16], F32),
         "oc%d" % _t: ("sbuf", [128, 8], U16), "og%d" % _t: ("sbuf", [128, 4], U16),
-        "oq%d" % _t: ("sbuf", [128, 8], U16), "om%d" % _t: ("sbuf", [128, 24], U16),
+        "ol%d" % _t: ("sbuf", [128, 32], U16),
     })
-    SEMAPHORES += ["x1_%d" % _t, "x2_%d" % _t, "own%d" % _t]
+    if _t < R - 1:
+        SCRATCH.update({"m%d" % _t: ("sbuf", [128, SP], CODE), "ms%d" % _t: ("sbuf", [128, SP], U8)})
+    SEMAPHORES += ["x1_%d" % _t, "x2_%d" % _t]
 
 
 def rank_program(g, core, T, topo):
@@ -92,7 +94,8 @@ def rank_program(g, core, T, topo):
         need("v", *deps)
         return did("v", V.tensor_copy(out, a))
 
-    def fill(ap, c):
+    def fill(ap, c, deps=()):
+        need("v", *deps)
         return did("v", V.memset(ap, c))
 
     def qmx(o, s, i, deps=()):
@@ -129,263 +132,233 @@ def rank_program(g, core, T, topo):
     def C(o, c0, c1, p0=0, p1=128, st=1):
         return T.cf[p0:p1, o + c0:o + c1:st]
 
+    engines = [e for e in topo.engines(core, T.cores[others[0]]) if all(e in topo.engines(core, T.cores[s]) for s in others)]
+    ne = len(engines)
     local = [0]
 
-    def send(src, dsts, rsem, deps):
+    def send(src, dsts, rsem, deps, use=engines):
         need("g", *deps)
-        mask = topo.mask(core, T.cores[others[0]])
         ids = []
         for s in others:
             rid, pid, _ = topo.addr(T.cores[s])
-            mask &= topo.mask(core, T.cores[s])
             ids.append(DstId(rid=rid, pnc=pid))
-        g.remote_dma_fused([RemoteDMATransfer(dst_ids=ids, dma_engine_mask=mask, remote_sem=sem[rsem], srcs=[src], dsts=dsts)],
-                           local_sem=sem["loc"])
-        local[0] += bin(mask).count("1")
+        g.remote_dma_fused([RemoteDMATransfer(dst_ids=ids, dma_engine_mask=sum(1 << e for e in use), remote_sem=sem[rsem],
+                                              srcs=[src], dsts=dsts)], local_sem=sem["loc"])
+        local[0] += len(use)
 
     u8, u32 = dt.uint8, dt.uint32
-    ne = len(topo.engines(core, T.cores[others[0]]))
 
     g.sync.dma_start(T.xt[:, 0:4 * A], T.x[:, :]).then_inc(sem.lx, 16)
-    S.dma_start(T.met[:, 0:2 * M], T.me[:, 0:2 * M]).then_inc(sem.lm, 16)
-    g.sync.dma_start(T.met[:, 2 * M:4 * M], T.me[:, 2 * M:4 * M]).then_inc(sem.lm, 16)
+    g.sync.dma_start(T.met[:, :], T.me[:, :]).then_inc(sem.lm, 16)
     g.sync.dma_start(T.wt[:, :], T.w[:, :]).then_inc(sem.lw, 16)
 
     small = {"allow_small_or_imprecise_dtypes": True}
-    cRow, cFour = cnew(32), cnew(4)
-    cNeg, cKeep, cE, cZero, c2k = cnew(HM), cnew(128), cnew(128), cnew(32), cnew(32)
-    cJ, cM16, cKb, cKc, cT0, cT1, cPl, cNp, cP31, cB = [cnew(n) for n in (1, 1, 3, 1, 1, 1, 3, 3, 1, 1)]
-    cMask, cTri, cNm = cnew(32), cnew(32), cnew(32)
+    cNeg, cW, cE, cTO, cZero, cJb, cNm, cRow = [cnew(n) for n in (HM, 128, 128, 64, 32, 32, 32, 32)]
+    cM16, cP31, cKb, cOf, cT0, cT1, cNp, cJf, cPb, cFour, c16, cP3 = [cnew(n) for n in (1, 1, 3, 1, 1, 1, 3, 1, 1, 4, 3, 3)]
+    WR, OH, G, KF, RW3, AB, PA, SG, WO = [new(n) for n in (128, 12, 16, 136, 8 * R, 3 * (SL + 1), 3, 3, 3)]
     i0 = io(T.ints[:, 0:1], [[0, 1]], 0, 1)
-    i5 = io(T.ce[:, 0:512], [[1, 512]], 0, 0, **small)
-    i4 = io(T.ce[:, 512:516], [[1, 4]], 0, 4, **small)
+    i1 = io(C(c16, 0, 3), [[16, 3]], 0, 0, **small)
+    i2 = io(C(cJb, 0, 32), [[0, 32]], 0, 1, **small)
     z0 = fill(T.xt[:, 4 * A:512], 0.0)
+    f0 = fill(C(cNeg, 0, HM), -1e29)
+    z1 = fill(T.et[:, :], 0.5)
     b0 = ts(T.ints[:, 1:2], T.ints[:, 0:1], 15, OP.bitwise_and, deps=[i0])
-    a0 = cp(C(cJ, 0, 1), T.ints[:, 0:1])
     b1 = ts(T.ints[:, 2:3], T.ints[:, 0:1], 31, OP.bitwise_and)
-    b2 = ts(T.ints[:, 3:4], T.ints[:, 0:1], 5, OP.arith_shift_right)
+    f2 = fill(C(cE, 0, 128, 0, 32), float(E))
     a1 = cp(C(cM16, 0, 1), T.ints[:, 1:2], [b0])
-    for c in range(3):
-        kKb = ts(C(cKb, c, c + 1), C(cM16, 0, 1), 16.0 * c + 0.5, OP.add, deps=[a1])
-    kOx = ts(T.offx[:, 0:2], C(cKb, 0, 2), -0.5, OP.add, deps=[kKb])
+    a2 = ts(C(cP31, 0, 1), T.ints[:, 2:3], -2.0, OP.mult, deps=[b1])
+    f3 = fill(C(cZero, 0, 32), 0.0)
+    kOx = ts(T.offx[:, 0:2], C(c16, 0, 2), C(cM16, 0, 1), OP.add, deps=[a1, i1])
+    kKb = ts(C(cKb, 0, 3), C(c16, 0, 3), C(cM16, 0, 1), OP.add, 0.5, OP.add)
+    kOf = ts(C(cOf, 0, 1), C(cM16, 0, 1), -15.0, OP.add, STEP, OP.mult)
+    fWR = fill(F(WR, 0, 128), 0.0)
     qx = qmx(T.xq[:, :], T.xs[:, :], T.xt[:, :], [("lx", 16), z0])
     o0, o1 = A * r, A * r + A
-    send(T.xq[:, 0:A].bitcast(u8), [T.q0[:, o0:o1].bitcast(u8)] * 3, "x0", [qx])
-    send(T.xs[:, 0:A], [T.qs0[:, o0:o1]] * 3, "x0", [qx])
-    i1 = io(T.ints[:, 16:48], [[1, 32]], 128, -1)
-    i2 = io(C(cRow, 0, 32), [[1, 32]], 0, 0, **small)
-    i3 = io(C(cFour, 0, 4), [[1, 4]], 1, 0, **small)
+    send(T.xq[:, 0:A].bitcast(u8), [T.q0[:, o0:o1].bitcast(u8)] * 3, "x0", [qx], engines[:ne // 2])
+    send(T.xs[:, 0:A], [T.qs0[:, o0:o1]] * 3, "x0", [qx], engines[ne // 2:])
+    i3 = io(T.ints[:, 8:136], [[1, 128]], 128, -1)
+    i4 = io(C(cRow, 0, 32), [[-2, 32]], 0, 0, **small)
+    i5 = io(C(cP3, 0, 3), [[32, 3]], 128, 3, **small)
+    i6 = io(C(cFour, 0, 4), [[1, 4]], 1, 0, **small)
+    need("g", z1)
+    i7 = did("g", g.affine_select(T.et[:, :], T.et[:, :], [[1, 516]], OP.is_equal, 0.0, -3, -4))
     own = cp(T.q0[:, o0:o1].bitcast(u32), T.xq[:, :].bitcast(u32).indirect(T.offx[:, 0:2]), [kOx, qx])
     owns = act(T.qs0[:, o0:o1], T.xs[:, :].indirect(T.offx[:, 0:2]), AF.Copy, [kOx, qx])
-    ke = []
-    for b in range(2):
-        x = act(T.ce[:, 520 + 512 * b:1032 + 512 * b], T.ce[:, 0:512], AF.Abs, [i4, i5], scale=-1.0, bias=T.ce[:, 512 + b:513 + b])
-        ke.append(act(T.et[:, 512 * b:512 * b + 512], T.ce[:, 520 + 512 * b:1032 + 512 * b], AF.Relu, [x], scale=-1.0, bias=0.5))
-    a2 = cp(C(cP31, 0, 1), T.ints[:, 2:3], [b1])
-    a3_ = ts(C(cB, 0, 1), T.ints[:, 3:4], 64.0, OP.mult, deps=[b2])
-    f0 = fill(C(cNeg, 0, HM), -1e29)
-    f1 = fill(C(cKeep, 0, 128), 1.0)
-    f2 = fill(C(cE, 0, 128), float(E))
-    f3 = fill(C(cZero, 0, 32), 0.0)
-    memd = qmx(T.m0[:, 128:128 + M], T.ms0[:, 128:128 + M], T.met[:, :], [("lm", 32)])
-    for b in (2, 3):
-        ke.append(ts(T.et[:, 512 * b:512 * b + 512], T.ce[:, 0:512], T.ce[:, 512 + b:513 + b], OP.is_equal, 0.5, OP.mult, deps=[i4, i5]))
-    f4 = fill(C(c2k, 0, 32), 2048.0)
-    need("v", f1)
-    f1 = fill(C(cKeep, 0, 128, st=16), 0.0)
-    b3 = ts(T.ints[:, 16:48], T.ints[:, 16:48], 15, OP.bitwise_and, deps=[i1])
-    kKc = ts(C(cKc, 0, 1), C(cJ, 0, 1), 2048.0, OP.add, deps=[a0])
-    kT = ts(C(cT0, 0, 1), C(cJ, 0, 1), -1.0, OP.mult, float(127 - SL), OP.add)
-    kT = ts(C(cT1, 0, 1), C(cJ, 0, 1), -1.0, OP.mult, float(127 - SL + E), OP.add)
-    kmask = ts(C(cMask, 0, 32), T.ints[:, 16:48], 0.0, OP.is_equal, 1e6, OP.mult, deps=[b3])
-    for h in range(3):
-        kPl = ts(C(cPl, h, h + 1), C(cB, 0, 1), C(cJ, 0, 1), OP.add, 128.0 + 32 * h, OP.add, deps=[a3_])
-    kTri = ts(C(cTri, 0, 32), C(cRow, 0, 32), C(cP31, 0, 1), OP.is_ge, 1e6, OP.mult, deps=[a2, i2])
-    kNm = ts(C(cNm, 0, 32), C(cMask, 0, 32), float(HM) - 1e6, OP.add, deps=[kmask])
-    kNp = ts(C(cNp, 0, 3), C(cPl, 0, 3), -127.0, OP.add, -2048.0, OP.mult, deps=[kPl])
-    ke = qmx(T.eq[:, :], T.es[:, :], T.et[:, :], ke)
-    WR, OH, A3, KF, K2, RW3 = new(128), new(12), new(3), new(136), new(136), new(16 * R)
-    fWR = fill(F(WR, 0, 128), 0.0)
+    kNm = act(C(cNm, 0, 32), C(cJb, 0, 32), AF.Copy, [i2], scale=1.0 / 1024, bias=float(HM + 1))
+    kJf = act(C(cJf, 0, 1), C(cJb, 0, 1), AF.Copy, scale=1.0 / 1024, bias=1.0)
+    kPb = act(C(cPb, 0, 1), C(cJb, 0, 1), AF.Copy, scale=-1.0 / 1024, bias=M * r - 0.5)
+    kT = act(C(cT0, 0, 1), C(cJb, 0, 1), AF.Copy, scale=-1.0 / 128, bias=(127.0 - SL) / 128)
+    kT = act(C(cT1, 0, 1), C(cJb, 0, 1), AF.Copy, scale=-1.0, bias=float(127 - SL + E))
     fKF = fill(F(KF, 128, 136), 0.0)
-    fK2 = fill(F(K2, 128, 136), -128.0)
-    fRW = fill(F(RW3, 0, 16 * R), -1e29)
+    fRW = fill(F(RW3, 0, 8 * R), -1e29)
+    f4 = fill(C(cTO, 32, 64), 1.0)
+    b3 = ts(T.ints[:, 8:136], T.ints[:, 8:136], 15, OP.bitwise_and, deps=[i3])
+    kTri = ts(C(cTO, 0, 32), C(cRow, 0, 32), C(cP31, 0, 1), OP.is_le, deps=[a2, i4])
+    kW = ts(C(cW, 0, 128), T.ints[:, 8:136], 1.0, OP.min, deps=[b3])
+    kPl = ts(F(AB, SL, 3 * (SL + 1), st=SL + 1), C(cP3, 0, 3), C(cP31, 0, 1), OP.add, deps=[i5])
+    kW = act(C(cW, 0, 128), C(cW, 0, 128), AF.Copy, [kW], scale=1024 * STEP + STEP, bias=-1024 * STEP)
+    kNp = act(C(cNp, 0, 3), F(AB, SL, 3 * (SL + 1), st=SL + 1), AF.Copy, [kPl], scale=-1024.0, bias=127.0 * 1024)
+    memd = qmx(T.m0[:, 128:SP], T.ms0[:, 128:SP], T.met[:, :], [("lm", 16)])
     kw = qmx(T.wq[:, :], T.ws[:, :], T.wt[:, :], [("lw", 16)])
+    for b in range(4):
+        ke = qmx(T.eq[:, 128 * b:128 * b + 128], T.es[:, 128 * b:128 * b + 128], T.et[:, 3 - b:515 - b], [i7])
 
-    qdeps = [own, owns, ("x0", 2 * ne * 3)]
+    qdeps = [own, owns, ("x0", ne * 3)]
     mdeps = [memd]
     scan_prev, cast_prev = [None, None], []
     for t in range(R):
-        land = T["land%d" % t]
-        m, ms, q, qs = T["m%d" % t], T["ms%d" % t], T["q%d" % t], T["qs%d" % t]
-        p, ps, s_, ss_ = T["p%d" % t], T["ps%d" % t], T["s%d" % t], T["ss%d" % t]
-        h = T["h%d" % t]
-        oc, og, oq, om = T["oc%d" % t], T["og%d" % t], T["oq%d" % t], T["om%d" % t]
         last = t == R - 1
+        land = T["land%d" % t]
+        q, qs, p, ps, h = T["q%d" % t], T["qs%d" % t], T["p%d" % t], T["ps%d" % t], T["h%d" % t]
+        m, ms, b0 = (q, qs, 128 + SP * r) if last else (T["m%d" % t], T["ms%d" % t], 0)
+        m0 = b0 + 128
+        oc, og, ol = T["oc%d" % t], T["og%d" % t], T["ol%d" % t]
         x1, x2 = "x1_%d" % t, "x2_%d" % t
-        RM, JK, CN, C0, C1 = new(M), new(M), new(1), new(1), new(1)
+        RM, JK, C0, C1 = new(M), new(M), new(1), new(1)
         half = [F(RM, k, M, st=2) for k in range(2)]
         top = [F(RM, M - 2 + k, M - 1 + k) for k in range(2)]
         rm = []
         for k in range(2):
-            rm.append(mm(T.pscore[:, 512 * k:512 * k + HM], q[:, 0:128], qs[:, 0:128], m[:, 128 + HM * k:128 + HM * k + HM],
-                         ms[:, 128 + HM * k:128 + HM * k + HM], True, True, qdeps + mdeps + [scan_prev[k]]))
+            rm.append(mm(T.pscore[:, 512 * k:512 * k + HM], q[:, 0:128], qs[:, 0:128], m[:, m0 + HM * k:m0 + HM * k + HM],
+                         ms[:, m0 + HM * k:m0 + HM * k + HM], True, True, qdeps + mdeps + [scan_prev[k]]))
         rm = [scan(half[k], T.pscore[:, 512 * k:512 * k + HM], C(cNeg, 0, HM), OP.max, OP.max, -1e29, [rm[k], f0]) for k in range(2)]
         scan_prev = rm
-        send(F(RM, M - 2, M), [land[:, 2 * r:2 * r + 2]] * 3, x1, rm)
+        send(F(RM, M - 2, M), [land[:, 4 * r:4 * r + 2]] * 3, x1, rm)
         for b in range(4):
             dq = mm(T.pblend[:, 512 * b:512 * b + 128], T.eq[:, 128 * b:128 * b + 128], T.es[:, 128 * b:128 * b + 128],
                     q[:, 0:128], qs[:, 0:128], True, False, [ke] + cast_prev)
-        B1, R1, R2, FC, K1, BA, NM, ME = new(32), new(128), new(128), new(1), new(1), new(1), new(32), new(1)
+        B1, R2, FC, BA, OW = new(32), new(128), new(1), new(1), new(32)
+        ME = land[:, 4 * r:4 * r + 1]
         c0_ = act(F(JK, 0, HM), half[0], AF.Sign, [rm[0]], scale=-1.0, bias=top[0], accum_out=F(C0, 0, 1))
         c1_ = act(F(JK, HM, M), half[1], AF.Sign, [rm[1]], scale=-1.0, bias=top[1], accum_out=F(C1, 0, 1))
-        k1 = ts(F(K1, 0, 1), top[1], top[0], OP.is_le, 1e5, OP.mult, deps=rm)
-        fc = ts(F(FC, 0, 1), top[1], top[0], OP.is_gt, 1e5, OP.mult)
-        mx = tt(F(ME, 0, 1), top[0], top[1], OP.max)
-        nm = ts(F(NM, 0, 32), C(cNm, 0, 32), F(K1, 0, 1), OP.add, deps=[k1, kNm])
-        ba = ts(F(BA, 0, 1), F(FC, 0, 1), F(C0, 0, 1), OP.add, deps=[fc, c0_])
-        bc = ts(F(B1, 0, 32), F(NM, 0, 32), F(C1, 0, 1), OP.add, F(BA, 0, 1), OP.min, deps=[nm, ba, c1_])
+        fc = ts(F(FC, 0, 1), top[1], top[0], OP.is_gt, 1e5, OP.mult, deps=rm)
+        mx = ts(land[:, 4 * r:4 * r + 2], F(RM, M - 2, M), top[0], OP.max, top[1], OP.max)
+        ba = ts(F(BA, 0, 1), F(C0, 0, 1), F(FC, 0, 1), OP.add, C(cJf, 0, 1), OP.add, deps=[fc, c0_, kJf])
+        bc = ts(F(B1, 0, 32), C(cNm, 0, 32), F(C1, 0, 1), OP.add, F(BA, 0, 1), OP.min, deps=[kNm, ba, c1_])
         for a in range(4):
-            x = tr(F(R1, 32 * a, 32 * a + 32, 0, 32), F(B1, 0, 32, 32 * a, 32 * a + 32), [bc])
-        k1 = ts(F(K1, 0, 1), F(K1, 0, 1), float(HM), OP.add)
-        x = scan(F(R2, 0, 128, 0, 32), C(cKeep, 0, 128, 0, 32), F(R1, 0, 128, 0, 32), OP.mult, OP.max, 0.0, [x, f1])
-        cn = ts(F(CN, 0, 1), F(C1, 0, 1), F(K1, 0, 1), OP.add, F(BA, 0, 1), OP.min, deps=[k1])
+            kf = tr(F(KF, 32 * a, 32 * a + 32, 0, 32), F(B1, 0, 32, 32 * a, 32 * a + 32), [bc])
+        x = scan(F(R2, 0, 128, 0, 32), C(cW, 0, 128, 0, 32), F(KF, 0, 128, 0, 32), OP.add, OP.max, 0.0, [kf, kW])
         for a in range(4):
-            lc = cp(oc[32 * a:32 * a + 32, 0:8], F(R2, 15, 128, 0, 32, 16), [x])
-        OW, KB = new(32), new(32)
-        ow = act(F(OW, 0, 32), C(cZero, 0, 32), AF.Identity, [f3, mx], bias=F(ME, 0, 1))
-        kb = act(F(KB, 0, 32), C(c2k, 0, 32), AF.Identity, [f4, cn, kKc], scale=F(CN, 0, 1), bias=C(cKc, 0, 1))
-        pl = act(T.places[:, t:t + 1], F(CN, 0, 1), AF.Copy, [cn], bias=float(M * r))
+            lc = ts(oc[32 * a:32 * a + 32, 0:8], F(R2, 15, 128, 0, 32, 16), C(cOf, 0, 1, 0, 32), OP.add, -1.0, OP.add, deps=[x])
+        ow = act(F(OW, 0, 32), C(cZero, 0, 32), AF.Identity, [f3, mx], bias=ME)
+        pl = act(T.places[:, t:t + 1], F(B1, 0, 1), AF.Identity, [bc, kPb], bias=C(cPb, 0, 1))
         if last:
             send(T.places[:, 0:R], [T.landp[:, R * r:R * r + R]] * 3, "xp", [pl])
-        pkc = cp(p[:, :].bitcast(u32), m[:, 128:128 + M].bitcast(u32).indirect(oc[:, 0:8]), [lc] + mdeps)
-        pks = act(ps[:, :], ms[:, 128:128 + M].indirect(oc[:, 0:8]), AF.Copy, [lc] + mdeps)
-        for a in range(4):
-            kf = tr(F(KF, 32 * a, 32 * a + 32, 0, 32), F(KB, 0, 32, 32 * a, 32 * a + 32), [kb])
+        for b in (1, 2, 3):
+            kk = act(F(KF, 0, 128, 32 * b, 32 * b + 32), F(KF, 0, 128, 0, 32), AF.Copy, [kf])
+        pkc = cp(p[:, :].bitcast(u32), m[:, m0:m0 + M].bitcast(u32).indirect(oc[:, 0:8]), [lc] + mdeps)
+        pks = act(ps[:, :], ms[:, m0:m0 + M].indirect(oc[:, 0:8]), AF.Copy, [lc] + mdeps)
         bl = []
         for b in range(4):
             bl.append(mm(T.pblend[:, 512 * b:512 * b + 128], T.eq[:, 128 * b:128 * b + 128], T.es[:, 128 * b:128 * b + 128],
                          p[:, :], ps[:, :], False, True, [pkc, pks]))
         cast_prev = []
-        for b in (0, 2):
-            cast_prev.append(act(h[:, b:512:4], T.pblend[:, 512 * b:512 * b + 128], AF.Copy, [bl[b]]))
-            cast_prev.append(cp(h[:, b + 1:512:4], T.pblend[:, 512 * b + 512:512 * b + 640], [bl[b + 1]]))
-        for b in (1, 2, 3):
-            kk = act(F(KF, 0, 128, 32 * b, 32 * b + 32), F(KF, 0, 128, 0, 32), AF.Copy, [kf])
-        nd = qmx(m[:, 0:128], ms[:, 0:128], h[:, :], cast_prev)
+        for b in range(4):
+            if last and b % 2:
+                cast_prev.append(cp(h[:, b:512:4], T.pblend[:, 512 * b:512 * b + 128], [bl[b]]))
+            else:
+                cast_prev.append(act(h[:, b:512:4], T.pblend[:, 512 * b:512 * b + 128], AF.Copy, [bl[b]]))
         if last:
-            k0 = 128 + 128 * r
-            send(m[:, 0:128].bitcast(u8), [q[:, k0:k0 + 128].bitcast(u8)] * 3, x2, [nd])
-            send(ms[:, 0:128], [qs[:, k0:k0 + 128]] * 3, x2, [nd])
-            need("y", nd)
-            g.sync.dma_start(q[:, k0:k0 + 128].bitcast(u8), m[:, 0:128].bitcast(u8)).then_inc(sem["own%d" % t], 16)
-            g.sync.dma_start(qs[:, k0:k0 + 128], ms[:, 0:128]).then_inc(sem["own%d" % t], 16)
+            nd = qmx(m[:, b0:m0], ms[:, b0:m0], h[:, :], cast_prev)
+            send(m[:, b0:m0].bitcast(u8), [m[:, b0:m0].bitcast(u8)] * 3, x2, [nd])
+            send(ms[:, b0:m0], [ms[:, b0:m0]] * 3, x2, [nd])
         x1 = (x1, 3 * ne)
-        MX, FL, MI, MR, AC, CS = new(1), new(1), new(32), new(128), new(3), new(128)
-        RW, S1, J3, BW, BT = RW3 + 16 * t, new(1), new(5), new(32), new(32)
-        lo = act(land[:, 2 * r:2 * r + 2], F(RM, M - 2, M), AF.Copy, [x1])
+        FL, MI, MR, AC, CS = new(1), new(32), new(128), new(3), new(128)
+        RW, S1, BW = RW3 + 8 * t, new(1), new(64)
+        rw = scan(F(RW, 1, 5), land[:, 0:16:4], land[:, 1:16:4], OP.max, OP.max, -1e29, [x1, mx, fRW])
         if r == 0:
-            x = red(F(MX, 0, 1), land[:, 2:8], OP.max, [x1])
-            mi = ts(F(MI, 0, 32), F(OW, 0, 32), F(MX, 0, 1), OP.is_ge, deps=[x, ow])
+            mi = ts(F(MI, 0, 32), F(OW, 0, 32), F(RW, 4, 5), OP.is_ge, deps=[rw, ow])
         elif r == 3:
-            x = red(F(MX, 0, 1), land[:, 0:6], OP.max, [x1])
-            mi = ts(F(MI, 0, 32), F(OW, 0, 32), F(MX, 0, 1), OP.is_gt, deps=[x, ow])
+            mi = ts(F(MI, 0, 32), F(OW, 0, 32), F(RW, 3, 4), OP.is_gt, deps=[rw, ow])
         elif r == 1:
-            x = red(F(MX, 0, 1), land[:, 4:8], OP.max, [x1])
-            x = ts(F(FL, 0, 1), land[:, 0:1], land[:, 1:2], OP.max, F(ME, 0, 1), OP.is_lt, deps=[mx])
-            mi = ts(F(MI, 0, 32), F(OW, 0, 32), F(MX, 0, 1), OP.is_ge, F(FL, 0, 1), OP.mult, deps=[x, ow])
+            x = ts(F(FL, 0, 1), land[:, 0:1], land[:, 1:2], OP.max, ME, OP.is_lt)
+            mi = ts(F(MI, 0, 32), F(OW, 0, 32), F(RW, 4, 5), OP.is_ge, F(FL, 0, 1), OP.mult, deps=[x, ow])
         else:
-            x = red(F(MX, 0, 1), land[:, 0:4], OP.max, [x1])
-            x = ts(F(FL, 0, 1), land[:, 6:7], land[:, 7:8], OP.max, F(ME, 0, 1), OP.is_le, deps=[mx])
-            mi = ts(F(MI, 0, 32), F(OW, 0, 32), F(MX, 0, 1), OP.is_gt, F(FL, 0, 1), OP.mult, deps=[x, ow])
+            x = ts(F(FL, 0, 1), land[:, 12:13], land[:, 13:14], OP.max, ME, OP.is_le)
+            mi = ts(F(MI, 0, 32), F(OW, 0, 32), F(RW, 2, 3), OP.is_gt, F(FL, 0, 1), OP.mult, deps=[x, ow])
         for a in range(4):
             x = tr(F(MR, 32 * a, 32 * a + 32, 0, 32), F(MI, 0, 32, 32 * a, 32 * a + 32), [mi])
         cs = scan(F(CS, 0, 128, 0, 32), F(MR, 0, 128, 0, 32), C(cE, 0, 128, 0, 32), OP.add, OP.min, 0.0, [x, f2])
-        for c in range(2):
-            ac = act(F(new(128), 0, 128, 0, 32), F(CS, 0, 128, 0, 32), AF.Sign, [cs, kKb], scale=-1.0, bias=C(cKb, c, c + 1, 0, 32),
-                     accum_out=F(AC, c, c + 1, 0, 32))
-        x = ts(F(K2, 0, 128, 0, 32), F(CS, 0, 128, 0, 32), C(cKb, 2, 3, 0, 32), OP.is_le, 2.0, OP.mult, deps=[cs, kKb])
-        rw = scan(F(RW, 1, 9), land[:, 0:8], C(cNeg, 0, 8), OP.max, OP.max, -1e29, [lo, x1, fRW])
-        av = red(F(AC, 2, 3, 0, 32), F(K2, 0, 129, 0, 32), OP.add, [x, fK2])
-        EQ, T1 = new(136), new(1)
-        s1 = act(F(J3, 0, 5), F(RW, 0, 9, st=2), AF.Sign, [rw], scale=-1.0, bias=F(RW, 8, 9), accum_out=F(S1, 0, 1))
-        bw = act(F(BW, 0, 32), C(cZero, 0, 32), AF.Identity, [s1], bias=F(S1, 0, 1))
-        for a in range(4):
-            lg = ts(og[32 * a:32 * a + 32, 0:3], F(AC, 0, 3, 0, 32), 0.5, OP.mult, 64.0, OP.add, deps=[ac, av])
+        TC, T1, PS = new(1), new(1), new(1)
+        s1 = act(F(new(4), 0, 4), F(RW, 0, 4), AF.Sign, [rw], scale=-1.0, bias=F(RW, 4, 5), accum_out=F(S1, 0, 1))
+        bw = act(F(BW, 0, 64), C(cTO, 0, 64), AF.Identity, [s1, kTri, f4], scale=F(S1, 0, 1))
+        for c in range(3):
+            ac = act(F(new(128), 0, 128, 0, 32), F(CS, 0, 128, 0, 32), AF.Sign, [cs, kKb], scale=-1.0,
+                     bias=C(cKb, c, c + 1, 0, 32), accum_out=F(AC, c, c + 1, 0, 32))
         if not last:
-            gc = cp(s_[:, :].bitcast(u32), m[:, :].bitcast(u32).indirect(og[:, 0:3]), [lg, nd])
-            gs = act(ss_[:, :], ms[:, :].indirect(og[:, 0:3]), AF.Copy, [lg, nd])
+            nd = qmx(m[:, b0:m0], ms[:, b0:m0], h[:, :], cast_prev)
+        x = tr(F(WR, 0, 32), F(BW, 0, 32), [bw, fWR])
+        x = tr(F(WR, 32, 64, 64, 128), F(BW, 32, 64, 0, 64))
+        x = tr(F(WR, 32, 64, 32, 64), F(BW, 32, 64, 0, 32))
+        oh = ts(F(OH, t, 12, st=3), C(cFour, 0, 4), F(S1, 0, 1), OP.is_equal, deps=[i6, s1])
+        if last:
+            lp = cp(T.landp[:, R * r:R * r + R], T.places[:, 0:R], [pl, ("xp", 3 * ne)])
+            gx = tt(F(G, 0, 12), F(OH, 0, 12), T.landp[:, 0:12], OP.mult, [oh, lp])
+        for a in range(4):
+            lg = ts(og[32 * a:32 * a + 32, 0:3], F(AC, 0, 3, 0, 32), 0.5, OP.mult, 64.0, OP.add, deps=[ac])
+        if not last:
             k0 = 128 + SL * r
-            send(s_[:, 0:E].bitcast(u8), [q[:, k0:k0 + E].bitcast(u8)] * 3, x2, [gc])
-            send(ss_[:, 0:E], [qs[:, k0:k0 + E]] * 3, x2, [gs])
-            need("y", gc, gs)
-            g.sync.dma_start(q[:, k0:k0 + SL].bitcast(u8), s_[:, :].bitcast(u8)).then_inc(sem["own%d" % t], 16)
-            g.sync.dma_start(qs[:, k0:k0 + SL], ss_[:, :]).then_inc(sem["own%d" % t], 16)
-        KG, AB, P, L, B2, R3, R4 = new(SL), new(3 * SL), new(1), new(1), new(32), new(128), new(128)
-        D, BM, R5, R6, LM, PS = new(3), new(96), new(96), new(96), new(24), new(1)
-        kg = act(F(KG, 0, SL), F(KF, 0, 136).indirect(og[:, 0:3]), AF.Copy, [kk, fKF, lg])
-        ab = [act(F(AB, SL * c, SL * c + SL), F(KG, 0, SL), AF.Abs, [kg, kNp], bias=C(cNp, c, c + 1)) for c in range(3)]
-        tc = act(F(EQ, 128, 129), F(S1, 0, 1), AF.Identity, [kT, s1], scale=float(SL), bias=C(cT0, 0, 1))
+            gc = cp(q[:, k0:k0 + SL].bitcast(u32), m[:, :].bitcast(u32).indirect(og[:, 0:3]), [lg, nd])
+            gs = act(qs[:, k0:k0 + SL], ms[:, :].indirect(og[:, 0:3]), AF.Copy, [lg, nd])
+            send(q[:, k0:k0 + E].bitcast(u8), [q[:, k0:k0 + E].bitcast(u8)] * 3, x2, [gc])
+            send(qs[:, k0:k0 + E], [qs[:, k0:k0 + E]] * 3, x2, [gs])
+            nd = [gc, gs]
+        else:
+            nd = [nd]
+        EQ, P, D, J, JT, JS, LM = new(128), new(1), new(3), new(128), new(128), new(128), new(32)
+        tc = act(F(TC, 0, 1), F(S1, 0, 1), AF.Identity, [kT, s1], scale=SL / 128.0, bias=C(cT0, 0, 1))
         tc = act(F(T1, 0, 1), F(S1, 0, 1), AF.Identity, scale=float(SL), bias=C(cT1, 0, 1))
         if last:
-            tc = act(F(PS, 0, 1), F(S1, 0, 1), AF.Copy, scale=128.0)
-        bt = ts(F(BT, 0, 32), C(cTri, 0, 32), F(S1, 0, 1), OP.min, deps=[s1, kTri])
-        for b in range(1, 4):
-            for a in range(b):
-                x = tr(F(WR, 32 + 32 * a, 64 + 32 * a, 32 * b, 32 * b + 32), F(BW, 0, 32, 32 * a, 32 * a + 32), [bw, fWR])
-        x = tr(F(WR, 0, 32), F(BT, 0, 32), [bt])
-        d = [red(F(D, c, c + 1), F(AB, SL * c, SL * c + SL), OP.min, [ab[c]]) for c in range(3)]
-        eq = ts(F(EQ, 0, 128), F(WR, 0, 128), F(S1, 0, 1), OP.is_equal, deps=[x])
-        pz = act(F(new(136), 0, 129), F(EQ, 0, 129), AF.Copy, [eq, tc], accum_out=F(P, 0, 1))
-        for c in range(3):
-            bm = ts(F(BM, 32 * c, 32 * c + 32), C(cMask, 0, 32), F(D, c, c + 1), OP.min, C(cPl, c, c + 1), OP.min, deps=[d[c]])
-        oh = ts(F(OH, t, 12, st=3), C(cFour, 0, 4), F(S1, 0, 1), OP.is_equal, deps=[i3])
-        y = tr(F(R5, 0, 96), F(BM, 0, 96), [bm])
-        z = ts(F(A3, t, t + 1), F(P, 0, 1), F(T1, 0, 1), OP.is_le, deps=[pz, tc])
-        y = scan(F(R6, 0, 96), C(cKeep, 0, 96), F(R5, 0, 96), OP.mult, OP.add, 0.0, [y])
-        z = ts(F(L, 0, 1), F(PS if last else P, 0, 1), F(A3, t, t + 1), OP.mult, C(cJ, 0, 1), OP.add, deps=[z])
-        lms = [act(F(LM, 6 * a, 6 * a + 6, 0, 32), F(R6, 15, 96, 32 * a, 32 * a + 32, 16), AF.Copy, [y]) for a in (2, 3)]
-        for a in range(2):
-            lmv = cp(F(LM, 6 * a, 6 * a + 6, 0, 32), F(R6, 15, 96, 32 * a, 32 * a + 32, 16), [y])
-        z = ts(F(B2, 0, 32), C(cMask, 0, 32), F(L, 0, 1), OP.min, deps=[z])
+            tc = act(F(PS, 0, 1), F(S1, 0, 1), AF.Copy, scale=float(SP), bias=float(128 - SP))
+        ab = [act(F(AB, (SL + 1) * c, (SL + 1) * c + SL), F(KF, 0, 136).indirect(og[:, 0:3]), AF.Abs, [kk, fKF, lg, kNp], scale=1024.0,
+                  bias=C(cNp, c, c + 1)) for c in range(3)]
+        x = tr(F(WR, 64, 96, 64, 96), F(BW, 32, 64, 32, 64))
+        x = tr(F(WR, 64, 96, 96, 128), F(BW, 32, 64, 0, 32))
+        x = tr(F(WR, 96, 128, 96, 128), F(BW, 32, 64, 64, 96))
         if last:
-            SG, AM = new(3), new(3)
-            lp = act(T.landp[:, R * r:R * r + R], T.places[:, 0:R], AF.Copy, [("xp", 3 * ne), pl])
-            sg = act(F(SG, 0, 3), F(A3, 0, 3), AF.Copy, [z], scale=2.0, bias=-1.0)
-            sg = act(F(AM, 0, 3), F(A3, 0, 3), AF.Copy, scale=1.0, bias=-1.0)
+            for c in range(R):
+                gw = red(F(G, 12 + c, 13 + c), F(G, c, 12, st=3), OP.add, [gx])
+        eq = ts(F(EQ, 0, 128), F(WR, 0, 128), F(S1, 0, 1), OP.is_equal, deps=[x])
+        d = [red(F(D, c, c + 1), F(AB, (SL + 1) * c, (SL + 1) * c + SL + 1), OP.min, [ab[c]]) for c in range(3)]
+        pz = act(F(new(128), 0, 128), F(EQ, 0, 128), AF.Identity, [eq, tc], bias=F(TC, 0, 1), accum_out=F(P, 0, 1))
+        for c in range(3):
+            jb = act(F(J, 32 + 32 * c, 64 + 32 * c), C(cZero, 0, 32), AF.Identity, [d[c]], bias=F(D, c, c + 1))
+        pa = ts(F(PA, t, t + 1), F(P, 0, 1), F(T1, 0, 1), OP.is_le, F(PS if last else P, 0, 1), OP.mult, deps=[pz])
+        x = ts(F(J, 0, 32), C(cJb, 0, 32), F(PA, t, t + 1), OP.add, deps=[pa])
+        sg = act(F(SG, t, t + 1), F(PA, t, t + 1), AF.Sign, [pa], bias=-0.5)
+        x = tr(F(JT, 0, 128), F(J, 0, 128), [x, jb])
+        if last:
+            for c in range(R):
+                w = act(F(WO, c, c + 1), F(G, 12 + c, 13 + c), AF.Identity, [sg, gw], scale=F(SG, c, c + 1), bias=-0.5)
+            need("y", w)
+            for c in range(R):
+                g.sync.dma_start(T.wi[c:c + 1, :], F(WO, c, c + 1)).then_inc(sem.out, 16)
+        x = scan(F(JS, 0, 128), C(cW, 0, 128), F(JT, 0, 128), OP.add, OP.max, 0.0, [x])
         for a in range(4):
-            x = tr(F(R3, 32 * a, 32 * a + 32, 0, 32), F(B2, 0, 32, 32 * a, 32 * a + 32), [z])
+            ls = act(F(LM, 2 * a, 2 * a + 2, 0, 32), F(JS, 15, 32, 32 * a, 32 * a + 32, 16), AF.Copy, [x])
+            lv = cp(F(LM, 8 + 6 * a, 14 + 6 * a, 0, 32), F(JS, 47, 128, 32 * a, 32 * a + 32, 16), [x])
         for b in range(4):
-            lm = cp(om[32 * b:32 * b + 32, :], F(LM, 0, 24, 0, 32), [lmv] + lms)
-        x = scan(F(R4, 0, 128, 0, 32), C(cKeep, 0, 128, 0, 32), F(R3, 0, 128, 0, 32), OP.mult, OP.add, 0.0, [x])
-        if not last:
-            m2, ms2, c0 = T["m%d" % (t + 1)], T["ms%d" % (t + 1)], 128
-        else:
+            ll = ts(ol[32 * b:32 * b + 32, :], F(LM, 0, 32, 0, 32), C(cOf, 0, 1, 0, 32), OP.add, deps=[ls, lv])
+        if t == R - 2:
+            m2, ms2, c0 = T["q%d" % (t + 1)], T["qs%d" % (t + 1)], 256 + SP * r
+        elif last:
             m2, ms2, c0 = T.m3, T.ms3, 0
-        mp = act(ms2[:, c0:c0 + M], ms[:, :].indirect(om[:, 0:24]), AF.Copy, [lm, nd] + mdeps)
-        for b in range(4):
-            lq = cp(oq[32 * b:32 * b + 32, :], F(R4, 15, 128, 0, 32, 16), [x])
-        mc = cp(m2[:, c0:c0 + M].bitcast(u32), m[:, :].bitcast(u32).indirect(om[:, 0:24]), [lm, nd] + mdeps)
+        else:
+            m2, ms2, c0 = T["m%d" % (t + 1)], T["ms%d" % (t + 1)], 128
+        mc = cp(m2[:, c0:c0 + M].bitcast(u32), m[:, b0:b0 + SP].bitcast(u32).indirect(ol[:, 8:32]), [ll] + nd + mdeps)
+        mp = act(ms2[:, c0:c0 + M], ms[:, b0:b0 + SP].indirect(ol[:, 8:32]), AF.Copy, [ll] + nd + mdeps)
         mdeps = [mc, mp]
         if last:
             need("y", mc, mp)
             g.sync.dma_start(T.oc[:, :], T.m3[:, :].bitcast(u8)).then_inc(sem.out, 16)
             for k in range(4):
                 g.sync.dma_start(T.osc[4 * k:4 * k + 4, :], T.ms3[32 * k:32 * k + 4, :]).then_inc(sem.out, 16)
-            G12, G3, W1, WO = new(12), new(3), new(3), new(3)
-            x = tt(F(G12, 0, 12), F(OH, 0, 12), T.landp[:, :], OP.mult, [oh, lp, ("xp", 3 * ne)])
-            for c in range(3):
-                w = red(F(G3, c, c + 1), F(G12, c, 12, st=3), OP.add, [x])
         q2, qs2 = T["q%d" % (t + 1)], T["qs%d" % (t + 1)]
-        ready = [lq, (x2, 2 * 3 * ne), ("own%d" % t, 32)] + qdeps
-        qdeps = [cp(q2[:, 0:128].bitcast(u32), q[:, :].bitcast(u32).indirect(oq[:, 0:8]), ready),
-                 act(qs2[:, 0:128], qs[:, :].indirect(oq[:, 0:8]), AF.Copy, ready)]
+        ready = [ll, (x2, 2 * 3 * ne)] + qdeps + nd
+        qdeps = [cp(q2[:, 0:128].bitcast(u32), q[:, :].bitcast(u32).indirect(ol[:, 0:8]), ready),
+                 act(qs2[:, 0:128], qs[:, :].indirect(ol[:, 0:8]), AF.Copy, ready)]
     y = mm(T.py[:, 0:128], T.wq[:, :], T.ws[:, :], T.q3[:, :], T.qs3[:, :], True, True, [kw] + qdeps)
-    x = tt(F(W1, 0, 3), F(G3, 0, 3), F(SG, 0, 3), OP.mult, [w, sg])
-    x = tt(F(WO, 0, 3), F(W1, 0, 3), F(AM, 0, 3), OP.add, [x])
     y = act(T.yo[:, :], T.py[:, 0:128], AF.Copy, [y])
-    need("y", x)
-    for c in range(R):
-        g.sync.dma_start(T.wi[c:c + 1, :], F(WO, c, c + 1)).then_inc(sem.out, 16)
     need("s", y)
     S.dma_start(T.y[:, :], T.yo[:, :]).then_inc(sem.out, 16)
     need("y", ("out", 16 * (1 + 4 + R + 1)))

@@ -6,18 +6,34 @@ HM = M // 2
 SL = 48
 SP = 128 + M
 QW, QL = 128 + 4 * SL, 128 + 4 * SP
-FW = 9000
+FW = 7500
 STEP = 4096.0
 CODE, U8, F32, BF, I32, U16 = "float8_e4m3fn_x4", "uint8", "float32", "bfloat16", "int32", "uint16"
+ORDER = """
+mm00 mm10 sc00 sc10 x10 dq00 dq10 dq20 dq30 c00 c10 fc0 mx0 ba0 bc00 bc10 kt00 kt10 ks00 ks10 lc00 lc10 lc30 lc20 ps0 kf30 kf10 ow0 pc0
+bl00 bl10 bl20 bl30 rw0 fl0 mi0 mt30 mt10 mt00 mt20 cs0 ca00 ca10 s10 ca20 ca30 bx0 b00 b10 b30 bw0 b20 ac00 ac10 tc00 nd0 k20 wr0 ac20
+eq0 tc10 kf00 kf20 pz0 lg00 lg10 lg20 lg30 gc0 ab20 ab00 ab10 gs0 x20 x30 lw0 pa0 d20 j00 d00 d10 jt0 js0 lm30 lm20 lm00 lm10
+ll30 ll20 ll10 ll00 mc0 qc00 qc10 mp0 qs00 qs10
+mm01 mm11 sc01 sc11 fc1 x11 dq01 dq11 dq21 dq31 c01 c11 mx1 ba1 bc01 bc11 kt11 kt01 ks11 ks01 lc01 lc31 lc11 lc21 pc1 kf11 kf01 ps1 kf21
+pl11 ow1 pl00 bl01 bl11 bl21 bl31 ca01 ca11 kw0 rw1 fl1 mi1 mt01 mt31 mt21 mt11 cs1 s11 ca21 ca31 b21 bw1 b01 bx1 b11 b31 ac01 ac11 nd1 k21
+wr1 ac21 eq1 lg31 lg21 lg01 lg11 tc11 kf31 tc01 pz1 gc1 ab01 ab21 ab11 gs1 pl01 x21 x31 pa1 d01 j01 d21 d11 jt1 js1 lm01 lm11 lm21 lm31
+ll31 ll21 ll11 ll01 oh1 mc1 qc11 qc01 mp1 pl10 qs01 qs11
+mm02 mm12 sc02 sc12 x12 dq02 dq12 dq22 dq32 c02 c12 fc2 ba2 mx2 bc02 bc12 kt12 kt02 ks12 ks02 lc12 lc32 lc22 lc02 pc2 kf12 pl12 kf22 pl02
+ps2 xp2 bl02 bl12 bl22 bl32 kf02 ca02 ca22 ow2 ca12 ca32 nd2 x22 x32 rw2 fl2 oh0 mi2 mt32 mt22 mt12 mt02 cs2 s12 b22 b02 tc22 b32 b12 bx2
+bw2 tc12 ac02 ac12 tc02 kf32 k22 wr2 lp2 ac22 eq2 pz2 lg12 lg32 lg02 lg22 ab12 ab02 ab22 sg1 pa2 j02 oh2 d12 d02 d22 jt2 js2 lm12 lm02 gx2
+sg2 lm32 lm22 w12 sg0 ll32 ll12 ll02 ll22 mc2 mp2 w22 w02 qs02 wi12 oc2 os12 wi22 os22 wi02 os32 os02 qc02 qc12 qs12 ym2 yc2 y2
+"""
 
 SCRATCH = {
     "xt": ("sbuf", [128, 512], BF), "xq": ("sbuf", [128, 128], CODE), "xs": ("sbuf", [128, 128], U8),
     "met": ("sbuf", [128, 4 * M], BF),
     "wt": ("sbuf", [128, 512], BF), "wq": ("sbuf", [128, 128], CODE), "ws": ("sbuf", [128, 128], U8),
     "et": ("sbuf", [128, 516], BF), "eq": ("sbuf", [128, 512], CODE), "es": ("sbuf", [128, 512], U8),
-    "ints": ("sbuf", [128, 136], I32),
+    "ints": ("sbuf", [128, 264], I32),
     "cf": ("sbuf", [128, 1100], F32),
-    "ff": ("sbuf", [128, FW], F32),
+    "ff": ("sbuf", [128, FW], F32), "fb": ("sbuf", [128, 1024], BF),
+    "kr": ("sbuf", [128, 2, 64], F32),
+    "ab": ("sbuf", [128, 3, SL + 32], F32), "jj": ("sbuf", [128, 4, SL + 32], F32), "lm": ("sbuf", [128, 4, 8], F32),
     "offx": ("sbuf", [128, 2], U16),
     "places": ("sbuf", [128, 4], F32), "landp": ("sbuf", [128, 12], F32),
     "yo": ("sbuf", [128, 128], F32),
@@ -38,7 +54,7 @@ for _t in range(R):
     })
     if _t < R - 1:
         SCRATCH.update({"m%d" % _t: ("sbuf", [128, SP], CODE), "ms%d" % _t: ("sbuf", [128, SP], U8)})
-    SEMAPHORES += ["x1_%d" % _t, "x2_%d" % _t]
+    SEMAPHORES += ["x1_%d" % _t, "x2_%d" % _t, "x3_%d" % _t]
 
 
 def rank_program(g, core, T, topo):
@@ -47,7 +63,7 @@ def rank_program(g, core, T, topo):
         return
     AF, OP, AXIS = ActivationFunctionType, AluOpType, AxisListType.X
     V, S, TE = g.vector, g.scalar, g.tensor
-    others = [(r + k) % 4 for k in (1, 2, 3)]
+    others = sorted([(r + k) % 4 for k in (1, 2, 3)], key=lambda s: topo.same_plane(topo.chip(core), topo.chip(T.cores[s])))
     queue = {"v": V, "s": S, "t": TE, "g": g, "y": g.sync}
     count = {"v": 0, "s": 0, "t": 0, "g": 0}
     seen = {k: {} for k in queue}
@@ -113,6 +129,10 @@ def rank_program(g, core, T, topo):
     def io(*a, **k):
         return did("g", g.iota(*a, **k))
 
+    def dma(qn, out, src, sm, deps=()):
+        need(qn, *deps)
+        queue[qn].dma_start(out, src).then_inc(sem[sm], 16)
+
     used, cpos = [0], [0]
 
     def new(n):
@@ -123,6 +143,9 @@ def rank_program(g, core, T, topo):
 
     def F(o, c0, c1, p0=0, p1=128, st=1):
         return T.ff[p0:p1, o + c0:o + c1:st]
+
+    def H(o, c0, c1, p0=0, p1=128):
+        return T.fb[p0:p1, o + c0:o + c1]
 
     def cnew(n):
         o = cpos[0]
@@ -136,230 +159,242 @@ def rank_program(g, core, T, topo):
     ne = len(engines)
     local = [0]
 
-    def send(src, dsts, rsem, deps, use=engines):
+    def send(src, dsts, rsem, deps):
         need("g", *deps)
         ids = []
         for s in others:
             rid, pid, _ = topo.addr(T.cores[s])
             ids.append(DstId(rid=rid, pnc=pid))
-        g.remote_dma_fused([RemoteDMATransfer(dst_ids=ids, dma_engine_mask=sum(1 << e for e in use), remote_sem=sem[rsem],
+        g.remote_dma_fused([RemoteDMATransfer(dst_ids=ids, dma_engine_mask=sum(1 << e for e in engines), remote_sem=sem[rsem],
                                               srcs=[src], dsts=dsts)], local_sem=sem["loc"])
-        local[0] += len(use)
+        local[0] += ne
 
     u8, u32 = dt.uint8, dt.uint32
 
-    g.sync.dma_start(T.xt[:, 0:4 * A], T.x[:, :]).then_inc(sem.lx, 16)
-    g.sync.dma_start(T.met[:, :], T.me[:, :]).then_inc(sem.lm, 16)
-    g.sync.dma_start(T.wt[:, :], T.w[:, :]).then_inc(sem.lw, 16)
+    dma("y", T.xt[:, 0:4 * A], T.x[:, :], "lx")
+    dma("y", T.met[:, :], T.me[:, :], "lm")
 
     small = {"allow_small_or_imprecise_dtypes": True}
-    cNeg, cW, cE, cTO, cZero, cJb, cNm, cRow = [cnew(n) for n in (HM, 128, 128, 64, 32, 32, 32, 32)]
-    cM16, cP31, cKb, cOf, cT0, cT1, cNp, cJf, cPb, cFour, c16, cP3 = [cnew(n) for n in (1, 1, 3, 1, 1, 1, 3, 1, 1, 4, 3, 3)]
-    WR, OH, G, KF, RW3, AB, PA, SG, WO = [new(n) for n in (128, 12, 16, 136, 8 * R, 3 * (SL + 1), 3, 3, 3)]
+    cNeg, cW, cTO, cZero, cJb, cNm, cRow = [cnew(n) for n in (HM, 128, 64, 32, 32, 32, 32)]
+    cM16, cP31, cKb, cOf, cT0, cT1, cNp, cJf, cPb, cFour, c16, cPl = [cnew(n) for n in (1, 1, 3, 1, 1, 1, 3, 1, 2, 4, 3, 3)]
+    OH, G, KF, RW3, PA, SG, WO = [new(n) for n in (12, 12, 136, 8 * R, 3, 3, 3)]
+    cE, MI, CS, WR, EQ, K2, MR, BW = 0, 128, 192, 384, 512, 640, 768, 896
     i0 = io(T.ints[:, 0:1], [[0, 1]], 0, 1)
     i1 = io(C(c16, 0, 3), [[16, 3]], 0, 0, **small)
+    i3 = io(T.ints[:, 8:136], [[1, 128]], 128, -1)
     i2 = io(C(cJb, 0, 32), [[0, 32]], 0, 1, **small)
+    i4 = io(C(cRow, 0, 32), [[-2, 32]], 0, 0, **small)
+    kPl = io(C(cPl, 0, 3), [[128, 3]], 128, 1, **small)
+    i6 = io(C(cFour, 0, 4), [[1, 4]], 1, 0, **small)
     z0 = fill(T.xt[:, 4 * A:512], 0.0)
-    f0 = fill(C(cNeg, 0, HM), -1e29)
-    z1 = fill(T.et[:, :], 0.5)
+    z1 = fill(T.et[:, :], 0.0)
     b0 = ts(T.ints[:, 1:2], T.ints[:, 0:1], 15, OP.bitwise_and, deps=[i0])
     b1 = ts(T.ints[:, 2:3], T.ints[:, 0:1], 31, OP.bitwise_and)
-    f2 = fill(C(cE, 0, 128, 0, 32), float(E))
+    f3 = fill(C(cZero, 0, 32), 0.0)
     a1 = cp(C(cM16, 0, 1), T.ints[:, 1:2], [b0])
     a2 = ts(C(cP31, 0, 1), T.ints[:, 2:3], -2.0, OP.mult, deps=[b1])
-    f3 = fill(C(cZero, 0, 32), 0.0)
     kOx = ts(T.offx[:, 0:2], C(c16, 0, 2), C(cM16, 0, 1), OP.add, deps=[a1, i1])
-    kKb = ts(C(cKb, 0, 3), C(c16, 0, 3), C(cM16, 0, 1), OP.add, 0.5, OP.add)
-    kOf = ts(C(cOf, 0, 1), C(cM16, 0, 1), -15.0, OP.add, STEP, OP.mult)
-    fWR = fill(F(WR, 0, 128), 0.0)
     qx = qmx(T.xq[:, :], T.xs[:, :], T.xt[:, :], [("lx", 16), z0])
     o0, o1 = A * r, A * r + A
-    send(T.xq[:, 0:A].bitcast(u8), [T.q0[:, o0:o1].bitcast(u8)] * 3, "x0", [qx], engines[:ne // 2])
-    send(T.xs[:, 0:A], [T.qs0[:, o0:o1]] * 3, "x0", [qx], engines[ne // 2:])
-    i3 = io(T.ints[:, 8:136], [[1, 128]], 128, -1)
-    i4 = io(C(cRow, 0, 32), [[-2, 32]], 0, 0, **small)
-    i5 = io(C(cP3, 0, 3), [[32, 3]], 128, 3, **small)
-    i6 = io(C(cFour, 0, 4), [[1, 4]], 1, 0, **small)
-    need("g", z1)
-    i7 = did("g", g.affine_select(T.et[:, :], T.et[:, :], [[1, 516]], OP.is_equal, 0.0, -3, -4))
+    send(T.xq[:, 0:A].bitcast(u8), [T.q0[:, o0:o1].bitcast(u8)] * 3, "x0", [qx])
+    send(T.xs[:, 0:A], [T.qs0[:, o0:o1]] * 3, "x0", [qx])
+    i7 = ts(T.et[:, 3:515:4], T.ints[:, 8:136], 128.0, OP.is_equal, 0.5, OP.mult, deps=[i3, z1])
     own = cp(T.q0[:, o0:o1].bitcast(u32), T.xq[:, :].bitcast(u32).indirect(T.offx[:, 0:2]), [kOx, qx])
     owns = act(T.qs0[:, o0:o1], T.xs[:, :].indirect(T.offx[:, 0:2]), AF.Copy, [kOx, qx])
     kNm = act(C(cNm, 0, 32), C(cJb, 0, 32), AF.Copy, [i2], scale=1.0 / 1024, bias=float(HM + 1))
     kJf = act(C(cJf, 0, 1), C(cJb, 0, 1), AF.Copy, scale=1.0 / 1024, bias=1.0)
-    kPb = act(C(cPb, 0, 1), C(cJb, 0, 1), AF.Copy, scale=-1.0 / 1024, bias=M * r - 0.5)
+    for k in range(2):
+        kPb = act(C(cPb, k, k + 1), C(cJb, 0, 1), AF.Copy, scale=-1.0 / 1024, bias=M * r - 0.5 - k * 64.0 / 1024)
     kT = act(C(cT0, 0, 1), C(cJb, 0, 1), AF.Copy, scale=-1.0 / 128, bias=(127.0 - SL) / 128)
     kT = act(C(cT1, 0, 1), C(cJb, 0, 1), AF.Copy, scale=-1.0, bias=float(127 - SL + E))
+    b3 = ts(T.ints[:, 136:264], T.ints[:, 8:136], 15, OP.bitwise_and)
+    for b in range(4):
+        ke = qmx(T.eq[:, 128 * b:128 * b + 128], T.es[:, 128 * b:128 * b + 128], T.et[:, 3 - b:515 - b], [i7])
+    kW = ts(C(cW, 0, 128), T.ints[:, 136:264], 1.0, OP.min, deps=[b3])
+    f0 = fill(C(cNeg, 0, HM), -1e29)
+    f2 = fill(H(cE, 0, 128, 0, 32), float(E))
+    kKb = ts(C(cKb, 0, 3), C(c16, 0, 3), C(cM16, 0, 1), OP.add, 0.5, OP.add)
+    kOf = ts(C(cOf, 0, 1), C(cM16, 0, 1), -15.0, OP.add, STEP, OP.mult)
+    fBW = fill(H(BW, 0, 128), 0.0)
+    fK2 = fill(H(K2, 96, 104, 0, 32), -64.0)
     fKF = fill(F(KF, 128, 136), 0.0)
     fRW = fill(F(RW3, 0, 8 * R), -1e29)
     f4 = fill(C(cTO, 32, 64), 1.0)
-    b3 = ts(T.ints[:, 8:136], T.ints[:, 8:136], 15, OP.bitwise_and, deps=[i3])
     kTri = ts(C(cTO, 0, 32), C(cRow, 0, 32), C(cP31, 0, 1), OP.is_le, deps=[a2, i4])
-    kW = ts(C(cW, 0, 128), T.ints[:, 8:136], 1.0, OP.min, deps=[b3])
-    kPl = ts(F(AB, SL, 3 * (SL + 1), st=SL + 1), C(cP3, 0, 3), C(cP31, 0, 1), OP.add, deps=[i5])
     kW = act(C(cW, 0, 128), C(cW, 0, 128), AF.Copy, [kW], scale=1024 * STEP + STEP, bias=-1024 * STEP)
-    kNp = act(C(cNp, 0, 3), F(AB, SL, 3 * (SL + 1), st=SL + 1), AF.Copy, [kPl], scale=-1024.0, bias=127.0 * 1024)
+    kNp = act(C(cNp, 0, 3), C(cPl, 0, 3), AF.Copy, [kPl], scale=-1024.0, bias=127.0 * 1024)
+    for c in range(3):
+        kNp = act(T.ab[:, c, SL:SL + 32], C(cZero, 0, 32), AF.Identity, [f3], bias=C(cPl, c, c + 1))
+    consts = [f0, f2, f3, f4, fBW, fK2, fKF, fRW, kKb, kOf, kTri, kW, kNm, kJf, kPb, kT, kNp, i6]
+    need("v", *consts)
+    need("s", *consts)
     memd = qmx(T.m0[:, 128:SP], T.ms0[:, 128:SP], T.met[:, :], [("lm", 16)])
-    kw = qmx(T.wq[:, :], T.ws[:, :], T.wt[:, :], [("lw", 16)])
-    for b in range(4):
-        ke = qmx(T.eq[:, 128 * b:128 * b + 128], T.es[:, 128 * b:128 * b + 128], T.et[:, 3 - b:515 - b], [i7])
 
-    qdeps = [own, owns, ("x0", ne * 3)]
-    mdeps = [memd]
-    scan_prev, cast_prev = [None, None], []
-    for t in range(R):
+    plan, done = {}, {}
+
+    def round_steps(t):
         last = t == R - 1
         land = T["land%d" % t]
         q, qs, p, ps, h = T["q%d" % t], T["qs%d" % t], T["p%d" % t], T["ps%d" % t], T["h%d" % t]
         m, ms, b0 = (q, qs, 128 + SP * r) if last else (T["m%d" % t], T["ms%d" % t], 0)
         m0 = b0 + 128
         oc, og, ol = T["oc%d" % t], T["og%d" % t], T["ol%d" % t]
-        x1, x2 = "x1_%d" % t, "x2_%d" % t
+        x1, x2, x3 = "x1_%d" % t, "x2_%d" % t, "x3_%d" % t
+
+        def step(name, fn, *a, **k):
+            deps = [(x, t) if isinstance(x, str) else x for x in k.pop("deps")]
+
+            def run():
+                assert not any(x in plan for x in deps)
+                return fn(*a, deps=[x[:2] if len(x) == 3 else done.get(x) for x in deps], **k)
+            plan[(name, t)] = run
+
+        def four(n, k=4):
+            return [n + str(a) for a in range(k)]
+
+        if t == 0:
+            newq, mem = [own + (0,), owns + (0,), ("x0", 2 * 3 * ne, 0)], [memd + (0,)]
+        else:
+            newq, mem = [(n, t - 1) for n in ("qc0", "qc1", "qs0", "qs1")], [("mc", t - 1), ("mp", t - 1)]
         RM, JK, C0, C1 = new(M), new(M), new(1), new(1)
         half = [F(RM, k, M, st=2) for k in range(2)]
         top = [F(RM, M - 2 + k, M - 1 + k) for k in range(2)]
-        rm = []
         for k in range(2):
-            rm.append(mm(T.pscore[:, 512 * k:512 * k + HM], q[:, 0:128], qs[:, 0:128], m[:, m0 + HM * k:m0 + HM * k + HM],
-                         ms[:, m0 + HM * k:m0 + HM * k + HM], True, True, qdeps + mdeps + [scan_prev[k]]))
-        rm = [scan(half[k], T.pscore[:, 512 * k:512 * k + HM], C(cNeg, 0, HM), OP.max, OP.max, -1e29, [rm[k], f0]) for k in range(2)]
-        scan_prev = rm
-        send(F(RM, M - 2, M), [land[:, 4 * r:4 * r + 2]] * 3, x1, rm)
-        for b in range(4):
-            dq = mm(T.pblend[:, 512 * b:512 * b + 128], T.eq[:, 128 * b:128 * b + 128], T.es[:, 128 * b:128 * b + 128],
-                    q[:, 0:128], qs[:, 0:128], True, False, [ke] + cast_prev)
-        B1, R2, FC, BA, OW = new(32), new(128), new(1), new(1), new(32)
+            step("mm%d" % k, mm, T.pscore[:, 512 * k:512 * k + HM], q[:, 0:128], qs[:, 0:128], m[:, m0 + HM * k:m0 + HM * k + HM],
+                 ms[:, m0 + HM * k:m0 + HM * k + HM], True, True, deps=newq + mem + [("sc%d" % k, t - 1)])
+            step("sc%d" % k, scan, half[k], T.pscore[:, 512 * k:512 * k + HM], C(cNeg, 0, HM), OP.max, OP.max, -1e29, deps=["mm%d" % k])
+        step("x1", send, F(RM, M - 2, M), [land[:, 4 * r:4 * r + 2]] * 3, x1, deps=["sc0", "sc1"])
+        B1, R2, FC, BA, OW = new(64), new(128), new(1), new(1), new(32)
         ME = land[:, 4 * r:4 * r + 1]
-        c0_ = act(F(JK, 0, HM), half[0], AF.Sign, [rm[0]], scale=-1.0, bias=top[0], accum_out=F(C0, 0, 1))
-        c1_ = act(F(JK, HM, M), half[1], AF.Sign, [rm[1]], scale=-1.0, bias=top[1], accum_out=F(C1, 0, 1))
-        fc = ts(F(FC, 0, 1), top[1], top[0], OP.is_gt, 1e5, OP.mult, deps=rm)
-        mx = ts(land[:, 4 * r:4 * r + 2], F(RM, M - 2, M), top[0], OP.max, top[1], OP.max)
-        ba = ts(F(BA, 0, 1), F(C0, 0, 1), F(FC, 0, 1), OP.add, C(cJf, 0, 1), OP.add, deps=[fc, c0_, kJf])
-        bc = ts(F(B1, 0, 32), C(cNm, 0, 32), F(C1, 0, 1), OP.add, F(BA, 0, 1), OP.min, deps=[kNm, ba, c1_])
+        step("c0", act, F(JK, 0, HM), half[0], AF.Sign, scale=-1.0, bias=top[0], accum_out=F(C0, 0, 1), deps=["sc0"])
+        step("c1", act, F(JK, HM, M), half[1], AF.Sign, scale=-1.0, bias=top[1], accum_out=F(C1, 0, 1), deps=["sc1"])
+        step("fc", ts, F(FC, 0, 1), top[1], top[0], OP.is_gt, 1e5, OP.mult, deps=["sc0", "sc1"])
+        step("mx", ts, land[:, 4 * r:4 * r + 2], F(RM, M - 2, M), top[0], OP.max, top[1], OP.max, deps=["sc0", "sc1"])
+        step("ba", ts, F(BA, 0, 1), F(C0, 0, 1), F(FC, 0, 1), OP.add, C(cJf, 0, 1), OP.add, deps=["fc", "c0"])
+        for k in range(2):
+            a, b = 64 * k, 64 * k + 64
+            step("bc%d" % k, ts, F(B1, 32 * k, 32 * k + 32, 0, 64), C(cNm, 0, 32, a, b), F(C1, 0, 1, a, b), OP.add, F(BA, 0, 1, a, b), OP.min,
+                 deps=["ba", "c1"])
+            step("kt%d" % k, tr, T.kr[0:32, :, 32 * k:32 * k + 32], F(B1, 0, 64, 32 * k, 32 * k + 32), deps=["bc0", "bc1"])
+            step("ks%d" % k, scan, F(R2, a, b, 0, 32), C(cW, 0, 64, 0, 32), T.kr[0:32, k, :], OP.add, OP.max, 0.0, deps=["kt0", "kt1"])
+            step("pl%d" % k, act, T.places[a:b, t:t + 1], F(B1, 32 * k, 32 * k + 1, 0, 64), AF.Identity, bias=C(cPb, k, k + 1, 0, 64),
+                 deps=["bc%d" % k])
         for a in range(4):
-            kf = tr(F(KF, 32 * a, 32 * a + 32, 0, 32), F(B1, 0, 32, 32 * a, 32 * a + 32), [bc])
-        x = scan(F(R2, 0, 128, 0, 32), C(cW, 0, 128, 0, 32), F(KF, 0, 128, 0, 32), OP.add, OP.max, 0.0, [kf, kW])
-        for a in range(4):
-            lc = ts(oc[32 * a:32 * a + 32, 0:8], F(R2, 15, 128, 0, 32, 16), C(cOf, 0, 1, 0, 32), OP.add, -1.0, OP.add, deps=[x])
-        ow = act(F(OW, 0, 32), C(cZero, 0, 32), AF.Identity, [f3, mx], bias=ME)
-        pl = act(T.places[:, t:t + 1], F(B1, 0, 1), AF.Identity, [bc, kPb], bias=C(cPb, 0, 1))
-        if last:
-            send(T.places[:, 0:R], [T.landp[:, R * r:R * r + R]] * 3, "xp", [pl])
-        for b in (1, 2, 3):
-            kk = act(F(KF, 0, 128, 32 * b, 32 * b + 32), F(KF, 0, 128, 0, 32), AF.Copy, [kf])
-        pkc = cp(p[:, :].bitcast(u32), m[:, m0:m0 + M].bitcast(u32).indirect(oc[:, 0:8]), [lc] + mdeps)
-        pks = act(ps[:, :], ms[:, m0:m0 + M].indirect(oc[:, 0:8]), AF.Copy, [lc] + mdeps)
-        bl = []
-        for b in range(4):
-            bl.append(mm(T.pblend[:, 512 * b:512 * b + 128], T.eq[:, 128 * b:128 * b + 128], T.es[:, 128 * b:128 * b + 128],
-                         p[:, :], ps[:, :], False, True, [pkc, pks]))
-        cast_prev = []
-        for b in range(4):
-            if last and b % 2:
-                cast_prev.append(cp(h[:, b:512:4], T.pblend[:, 512 * b:512 * b + 128], [bl[b]]))
+            step("lc%d" % a, ts, oc[32 * a:32 * a + 32, 0:8], F(R2, 15, 128, 0, 32, 16), C(cOf, 0, 1, 0, 32), OP.add, -1.0, OP.add,
+                 deps=["ks0", "ks1"])
+            step("kf%d" % a, act, F(KF, 0, 128, 32 * a, 32 * a + 32), T.kr[0:32, :, :], AF.Copy, deps=["kt0", "kt1"])
+            bank = T.pblend[:, 512 * a:512 * a + 128]
+            e, es = T.eq[:, 128 * a:128 * a + 128], T.es[:, 128 * a:128 * a + 128]
+            step("dq%d" % a, mm, bank, e, es, q[:, 0:128], qs[:, 0:128], True, False, deps=newq + [ke + (0,), ("ca%d" % a, t - 1)])
+            step("bl%d" % a, mm, bank, e, es, p[:, :], ps[:, :], False, True, deps=["pc", "ps"])
+            if last and a % 2:
+                step("ca%d" % a, cp, h[:, a:512:4], bank, deps=["bl%d" % a])
             else:
-                cast_prev.append(act(h[:, b:512:4], T.pblend[:, 512 * b:512 * b + 128], AF.Copy, [bl[b]]))
+                step("ca%d" % a, act, h[:, a:512:4], bank, AF.Copy, deps=["bl%d" % a])
+        step("ow", act, F(OW, 0, 32), C(cZero, 0, 32), AF.Identity, bias=ME, deps=["mx"])
+        step("pc", cp, p[:, :].bitcast(u32), m[:, m0:m0 + M].bitcast(u32).indirect(oc[:, 0:8]), deps=four("lc") + mem)
+        step("ps", act, ps[:, :], ms[:, m0:m0 + M].indirect(oc[:, 0:8]), AF.Copy, deps=four("lc") + mem)
+        step("nd", qmx, m[:, b0:m0], ms[:, b0:m0], h[:, :], deps=four("ca"))
+        FL, AC, S1, TC, T1, PS, P = new(1), new(3), new(1), new(1), new(1), new(1), new(1)
+        RW = RW3 + 8 * t
+        got = (x1, 3 * ne, 0)
+        step("rw", scan, F(RW, 1, 5), land[:, 0:16:4], land[:, 1:16:4], OP.max, OP.max, -1e29, deps=[got, "mx"])
+        if r == 1:
+            step("fl", ts, F(FL, 0, 1), land[:, 0:1], land[:, 1:2], OP.max, ME, OP.is_lt, deps=[got, "mx"])
+        if r == 2:
+            step("fl", ts, F(FL, 0, 1), land[:, 12:13], land[:, 13:14], OP.max, ME, OP.is_le, deps=[got, "mx"])
+        c, op = ((4, OP.is_ge), (4, OP.is_ge), (2, OP.is_gt), (3, OP.is_gt))[r]
+        step("mi", ts, H(MI, 0, 32), F(OW, 0, 32), F(RW, c, c + 1), op, *((F(FL, 0, 1), OP.mult) if r in (1, 2) else ()), deps=["rw", "fl", "ow"])
+        for a in range(4):
+            step("mt%d" % a, tr, H(MR, 32 * a, 32 * a + 32, 0, 32), H(MI, 0, 32, 32 * a, 32 * a + 32), deps=["mi"])
+            step("lg%d" % a, ts, og[32 * a:32 * a + 32, 0:3], F(AC, 0, 3, 0, 32), 0.5, OP.mult, 64.0, OP.add, deps=four("ac", 3))
+        step("cs", scan, H(CS, 0, 128, 0, 32), H(MR, 0, 128, 0, 32), H(cE, 0, 128, 0, 32), OP.add, OP.min, 0.0, deps=four("mt"))
+        for c in range(2):
+            step("ac%d" % c, act, F(new(128), 0, 128, 0, 32), H(CS, 0, 128, 0, 32), AF.Sign, scale=-1.0, bias=C(cKb, c, c + 1, 0, 32),
+                 accum_out=F(AC, c, c + 1, 0, 32), deps=["cs"])
+        step("k2", ts, H(K2, 0, 96, 0, 32), H(CS, 32, 128, 0, 32), C(cKb, 2, 3, 0, 32), OP.is_le, 2.0, OP.mult, deps=["cs"])
+        step("ac2", red, F(AC, 2, 3, 0, 32), H(K2, 0, 97, 0, 32), OP.add, deps=["k2"])
         if last:
-            nd = qmx(m[:, b0:m0], ms[:, b0:m0], h[:, :], cast_prev)
-            send(m[:, b0:m0].bitcast(u8), [m[:, b0:m0].bitcast(u8)] * 3, x2, [nd])
-            send(ms[:, b0:m0], [ms[:, b0:m0]] * 3, x2, [nd])
-        x1 = (x1, 3 * ne)
-        FL, MI, MR, AC, CS = new(1), new(32), new(128), new(3), new(128)
-        RW, S1, BW = RW3 + 8 * t, new(1), new(64)
-        rw = scan(F(RW, 1, 5), land[:, 0:16:4], land[:, 1:16:4], OP.max, OP.max, -1e29, [x1, mx, fRW])
-        if r == 0:
-            mi = ts(F(MI, 0, 32), F(OW, 0, 32), F(RW, 4, 5), OP.is_ge, deps=[rw, ow])
-        elif r == 3:
-            mi = ts(F(MI, 0, 32), F(OW, 0, 32), F(RW, 3, 4), OP.is_gt, deps=[rw, ow])
-        elif r == 1:
-            x = ts(F(FL, 0, 1), land[:, 0:1], land[:, 1:2], OP.max, ME, OP.is_lt)
-            mi = ts(F(MI, 0, 32), F(OW, 0, 32), F(RW, 4, 5), OP.is_ge, F(FL, 0, 1), OP.mult, deps=[x, ow])
+            step("x2", send, m[:, b0:m0].bitcast(u8), [m[:, b0:m0].bitcast(u8)] * 3, x2, deps=["nd"])
+            step("x3", send, ms[:, b0:m0], [ms[:, b0:m0]] * 3, x3, deps=["nd"])
         else:
-            x = ts(F(FL, 0, 1), land[:, 12:13], land[:, 13:14], OP.max, ME, OP.is_le)
-            mi = ts(F(MI, 0, 32), F(OW, 0, 32), F(RW, 2, 3), OP.is_gt, F(FL, 0, 1), OP.mult, deps=[x, ow])
-        for a in range(4):
-            x = tr(F(MR, 32 * a, 32 * a + 32, 0, 32), F(MI, 0, 32, 32 * a, 32 * a + 32), [mi])
-        cs = scan(F(CS, 0, 128, 0, 32), F(MR, 0, 128, 0, 32), C(cE, 0, 128, 0, 32), OP.add, OP.min, 0.0, [x, f2])
-        TC, T1, PS = new(1), new(1), new(1)
-        s1 = act(F(new(4), 0, 4), F(RW, 0, 4), AF.Sign, [rw], scale=-1.0, bias=F(RW, 4, 5), accum_out=F(S1, 0, 1))
-        bw = act(F(BW, 0, 64), C(cTO, 0, 64), AF.Identity, [s1, kTri, f4], scale=F(S1, 0, 1))
-        for c in range(3):
-            ac = act(F(new(128), 0, 128, 0, 32), F(CS, 0, 128, 0, 32), AF.Sign, [cs, kKb], scale=-1.0,
-                     bias=C(cKb, c, c + 1, 0, 32), accum_out=F(AC, c, c + 1, 0, 32))
-        if not last:
-            nd = qmx(m[:, b0:m0], ms[:, b0:m0], h[:, :], cast_prev)
-        x = tr(F(WR, 0, 32), F(BW, 0, 32), [bw, fWR])
-        x = tr(F(WR, 32, 64, 64, 128), F(BW, 32, 64, 0, 64))
-        x = tr(F(WR, 32, 64, 32, 64), F(BW, 32, 64, 0, 32))
-        oh = ts(F(OH, t, 12, st=3), C(cFour, 0, 4), F(S1, 0, 1), OP.is_equal, deps=[i6, s1])
-        if last:
-            lp = cp(T.landp[:, R * r:R * r + R], T.places[:, 0:R], [pl, ("xp", 3 * ne)])
-            gx = tt(F(G, 0, 12), F(OH, 0, 12), T.landp[:, 0:12], OP.mult, [oh, lp])
-        for a in range(4):
-            lg = ts(og[32 * a:32 * a + 32, 0:3], F(AC, 0, 3, 0, 32), 0.5, OP.mult, 64.0, OP.add, deps=[ac])
-        if not last:
             k0 = 128 + SL * r
-            gc = cp(q[:, k0:k0 + SL].bitcast(u32), m[:, :].bitcast(u32).indirect(og[:, 0:3]), [lg, nd])
-            gs = act(qs[:, k0:k0 + SL], ms[:, :].indirect(og[:, 0:3]), AF.Copy, [lg, nd])
-            send(q[:, k0:k0 + E].bitcast(u8), [q[:, k0:k0 + E].bitcast(u8)] * 3, x2, [gc])
-            send(qs[:, k0:k0 + E], [qs[:, k0:k0 + E]] * 3, x2, [gs])
-            nd = [gc, gs]
-        else:
-            nd = [nd]
-        EQ, P, D, J, JT, JS, LM = new(128), new(1), new(3), new(128), new(128), new(128), new(32)
-        tc = act(F(TC, 0, 1), F(S1, 0, 1), AF.Identity, [kT, s1], scale=SL / 128.0, bias=C(cT0, 0, 1))
-        tc = act(F(T1, 0, 1), F(S1, 0, 1), AF.Identity, scale=float(SL), bias=C(cT1, 0, 1))
+            step("gc", cp, q[:, k0:k0 + SL].bitcast(u32), m[:, :].bitcast(u32).indirect(og[:, 0:3]), deps=four("lg") + ["nd"])
+            step("gs", act, qs[:, k0:k0 + SL], ms[:, :].indirect(og[:, 0:3]), AF.Copy, deps=four("lg") + ["nd"])
+            step("x2", send, q[:, k0:k0 + E].bitcast(u8), [q[:, k0:k0 + E].bitcast(u8)] * 3, x2, deps=["gc"])
+            step("x3", send, qs[:, k0:k0 + E], [qs[:, k0:k0 + E]] * 3, x3, deps=["gs"])
+        JT, JS = new(128), new(128)
+        step("s1", act, F(new(4), 0, 4), F(RW, 0, 4), AF.Sign, scale=-1.0, bias=F(RW, 4, 5), accum_out=F(S1, 0, 1), deps=["rw"])
+        step("tc0", act, F(TC, 0, 1), F(S1, 0, 1), AF.Identity, scale=SL / 128.0, bias=C(cT0, 0, 1), deps=["s1"])
+        step("tc1", act, F(T1, 0, 1), F(S1, 0, 1), AF.Identity, scale=float(SL), bias=C(cT1, 0, 1), deps=["s1"])
         if last:
-            tc = act(F(PS, 0, 1), F(S1, 0, 1), AF.Copy, scale=float(SP), bias=float(128 - SP))
-        ab = [act(F(AB, (SL + 1) * c, (SL + 1) * c + SL), F(KF, 0, 136).indirect(og[:, 0:3]), AF.Abs, [kk, fKF, lg, kNp], scale=1024.0,
-                  bias=C(cNp, c, c + 1)) for c in range(3)]
-        x = tr(F(WR, 64, 96, 64, 96), F(BW, 32, 64, 32, 64))
-        x = tr(F(WR, 64, 96, 96, 128), F(BW, 32, 64, 0, 32))
-        x = tr(F(WR, 96, 128, 96, 128), F(BW, 32, 64, 64, 96))
-        if last:
-            for c in range(R):
-                gw = red(F(G, 12 + c, 13 + c), F(G, c, 12, st=3), OP.add, [gx])
-        eq = ts(F(EQ, 0, 128), F(WR, 0, 128), F(S1, 0, 1), OP.is_equal, deps=[x])
-        d = [red(F(D, c, c + 1), F(AB, (SL + 1) * c, (SL + 1) * c + SL + 1), OP.min, [ab[c]]) for c in range(3)]
-        pz = act(F(new(128), 0, 128), F(EQ, 0, 128), AF.Identity, [eq, tc], bias=F(TC, 0, 1), accum_out=F(P, 0, 1))
+            step("tc2", act, F(PS, 0, 1), F(S1, 0, 1), AF.Copy, scale=float(SP), bias=float(128 - SP), deps=["s1"])
+        step("bw", act, H(BW, 0, 32), C(cTO, 0, 32), AF.Identity, scale=F(S1, 0, 1), deps=["s1"])
+        step("bx", act, H(BW, 32, 64, 64, 128), C(cTO, 32, 64, 0, 64), AF.Identity, scale=F(S1, 0, 1, 0, 64), deps=["s1"])
+        for k, (a, b, c) in enumerate(((0, 1, 1), (1, 2, 2), (0, 3, 2), (2, 3, 3))):
+            step("b%d" % k, act, H(BW, 32 * c, 32 * c + 32, 32 * b, 32 * b + 32), C(cTO, 32, 64, 32 * a, 32 * a + 32), AF.Identity,
+                 scale=F(S1, 0, 1, 32 * a, 32 * a + 32), deps=["s1"])
+        step("wr", tr, H(WR, 0, 128), H(BW, 0, 128), deps=["bw", "bx"] + four("b"))
+        step("eq", ts, H(EQ, 0, 128), H(WR, 0, 128), F(S1, 0, 1), OP.is_equal, deps=["wr"])
+        step("pz", act, F(new(128), 0, 128), H(EQ, 0, 128), AF.Identity, bias=F(TC, 0, 1), accum_out=F(P, 0, 1), deps=["eq", "tc0"])
+        step("pa", ts, F(PA, t, t + 1), F(P, 0, 1), F(T1, 0, 1), OP.is_le, F(PS if last else P, 0, 1), OP.mult, deps=["pz", "tc1", "tc2"])
+        step("j0", ts, T.jj[:, 0, SL:SL + 32], C(cJb, 0, 32), F(PA, t, t + 1), OP.add, deps=["pa"])
         for c in range(3):
-            jb = act(F(J, 32 + 32 * c, 64 + 32 * c), C(cZero, 0, 32), AF.Identity, [d[c]], bias=F(D, c, c + 1))
-        pa = ts(F(PA, t, t + 1), F(P, 0, 1), F(T1, 0, 1), OP.is_le, F(PS if last else P, 0, 1), OP.mult, deps=[pz])
-        x = ts(F(J, 0, 32), C(cJb, 0, 32), F(PA, t, t + 1), OP.add, deps=[pa])
-        sg = act(F(SG, t, t + 1), F(PA, t, t + 1), AF.Sign, [pa], bias=-0.5)
-        x = tr(F(JT, 0, 128), F(J, 0, 128), [x, jb])
-        if last:
-            for c in range(R):
-                w = act(F(WO, c, c + 1), F(G, 12 + c, 13 + c), AF.Identity, [sg, gw], scale=F(SG, c, c + 1), bias=-0.5)
-            need("y", w)
-            for c in range(R):
-                g.sync.dma_start(T.wi[c:c + 1, :], F(WO, c, c + 1)).then_inc(sem.out, 16)
-        x = scan(F(JS, 0, 128), C(cW, 0, 128), F(JT, 0, 128), OP.add, OP.max, 0.0, [x])
+            step("ab%d" % c, act, T.ab[:, c, 0:SL], F(KF, 0, 136).indirect(og[:, 0:3]), AF.Abs, scale=1024.0, bias=C(cNp, c, c + 1),
+                 deps=four("lg") + four("kf"))
+            step("d%d" % c, scan, T.jj[:, c + 1, :], T.ab[:, c, :], T.ab[:, c, :], OP.min, OP.min, 1e9, deps=["ab%d" % c])
+        step("jt", tr, F(JT, 0, 128), T.jj[:, :, SL:SL + 32], deps=["j0"] + four("d", 3))
+        step("js", scan, F(JS, 0, 128), C(cW, 0, 128), F(JT, 0, 128), OP.add, OP.max, 0.0, deps=["jt"])
         for a in range(4):
-            ls = act(F(LM, 2 * a, 2 * a + 2, 0, 32), F(JS, 15, 32, 32 * a, 32 * a + 32, 16), AF.Copy, [x])
-            lv = cp(F(LM, 8 + 6 * a, 14 + 6 * a, 0, 32), F(JS, 47, 128, 32 * a, 32 * a + 32, 16), [x])
-        for b in range(4):
-            ll = ts(ol[32 * b:32 * b + 32, :], F(LM, 0, 32, 0, 32), C(cOf, 0, 1, 0, 32), OP.add, deps=[ls, lv])
+            out, src = T.lm[0:32, :, 2 * a:2 * a + 2], F(JS, 15, 128, 32 * a, 32 * a + 32, 16)
+            if a < 2:
+                step("lm%d" % a, cp, out, src, deps=["js"])
+            else:
+                step("lm%d" % a, act, out, src, AF.Copy, deps=["js"])
+            step("ll%d" % a, ts, ol[32 * a:32 * a + 32, :], T.lm[0:32, :, :], C(cOf, 0, 1, 0, 32), OP.add, deps=four("lm"))
         if t == R - 2:
             m2, ms2, c0 = T["q%d" % (t + 1)], T["qs%d" % (t + 1)], 256 + SP * r
         elif last:
             m2, ms2, c0 = T.m3, T.ms3, 0
         else:
             m2, ms2, c0 = T["m%d" % (t + 1)], T["ms%d" % (t + 1)], 128
-        mc = cp(m2[:, c0:c0 + M].bitcast(u32), m[:, b0:b0 + SP].bitcast(u32).indirect(ol[:, 8:32]), [ll] + nd + mdeps)
-        mp = act(ms2[:, c0:c0 + M], ms[:, b0:b0 + SP].indirect(ol[:, 8:32]), AF.Copy, [ll] + nd + mdeps)
-        mdeps = [mc, mp]
-        if last:
-            need("y", mc, mp)
-            g.sync.dma_start(T.oc[:, :], T.m3[:, :].bitcast(u8)).then_inc(sem.out, 16)
-            for k in range(4):
-                g.sync.dma_start(T.osc[4 * k:4 * k + 4, :], T.ms3[32 * k:32 * k + 4, :]).then_inc(sem.out, 16)
+        d = four("ll") + ["nd"] + mem
+        step("mc", cp, m2[:, c0:c0 + M].bitcast(u32), m[:, b0:b0 + SP].bitcast(u32).indirect(ol[:, 8:32]), deps=d)
+        step("mp", act, ms2[:, c0:c0 + M], ms[:, b0:b0 + SP].indirect(ol[:, 8:32]), AF.Copy, deps=d)
         q2, qs2 = T["q%d" % (t + 1)], T["qs%d" % (t + 1)]
-        ready = [ll, (x2, 2 * 3 * ne)] + qdeps + nd
-        qdeps = [cp(q2[:, 0:128].bitcast(u32), q[:, :].bitcast(u32).indirect(ol[:, 0:8]), ready),
-                 act(qs2[:, 0:128], qs[:, :].indirect(ol[:, 0:8]), AF.Copy, ready)]
-    y = mm(T.py[:, 0:128], T.wq[:, :], T.ws[:, :], T.q3[:, :], T.qs3[:, :], True, True, [kw] + qdeps)
-    y = act(T.yo[:, :], T.py[:, 0:128], AF.Copy, [y])
-    need("s", y)
-    S.dma_start(T.y[:, :], T.yo[:, :]).then_inc(sem.out, 16)
+        d = four("ll") + newq + ["nd", "gc", "gs"]
+        for k in range(2):
+            step("qc%d" % k, cp, q2[:, 64 * k:64 * k + 64].bitcast(u32), q[:, :].bitcast(u32).indirect(ol[:, 4 * k:4 * k + 4]),
+                 deps=d + [(x2, 3 * ne, 0)])
+        step("qs0", act, qs2[:, 0:64], qs[:, :].indirect(ol[:, 0:4]), AF.Copy, deps=d + [(x3, 3 * ne, 0)])
+        step("qs1", cp, qs2[:, 64:128], qs[:, :].indirect(ol[:, 4:8]), deps=d + [(x3, 3 * ne, 0)])
+        step("oh", ts, F(OH, t, 12, st=3), C(cFour, 0, 4), F(S1, 0, 1), OP.is_equal, deps=["s1"])
+        step("sg", act, F(SG, t, t + 1), F(PA, t, t + 1), AF.Sign, bias=-0.5, deps=["pa"])
+        if t == 0:
+            step("lw", dma, "y", T.wt[:, :], T.w[:, :], "lw", deps=[got])
+            step("kw", qmx, T.wq[:, :], T.ws[:, :], T.wt[:, :], deps=[("lw", 16, 0)])
+        if last:
+            pl = [(n, c) for c in range(R) for n in ("pl0", "pl1")]
+            step("xp", send, T.places[:, 0:R], [T.landp[:, R * r:R * r + R]] * 3, "xp", deps=pl)
+            step("lp", cp, T.landp[:, R * r:R * r + R], T.places[:, 0:R], deps=pl + [("xp", 3 * ne, 0)])
+            step("gx", tt, F(G, 0, 12), F(OH, 0, 12), T.landp[:, 0:12], OP.mult, deps=[("oh", c) for c in range(R)] + ["lp"])
+            for c in range(R):
+                step("w%d" % c, act, F(new(4), 0, 4), F(G, c, 12, st=3), AF.Identity, scale=F(SG, c, c + 1), bias=-0.125,
+                     accum_out=F(WO, c, c + 1), deps=[("sg", c), "gx"])
+                step("wi%d" % c, dma, "y", T.wi[c:c + 1, :], F(WO, c, c + 1), "out", deps=["w%d" % c])
+            step("oc", dma, "y", T.oc[:, :], T.m3[:, :].bitcast(u8), "out", deps=["mc"])
+            for k in range(4):
+                step("os%d" % k, dma, "y", T.osc[4 * k:4 * k + 4, :], T.ms3[32 * k:32 * k + 4, :], "out", deps=["mp"])
+            step("ym", mm, T.py[:, 0:128], T.wq[:, :], T.ws[:, :], T.q3[:, :], T.qs3[:, :], True, True, deps=[("kw", 0), "qc0", "qc1", "qs0", "qs1"])
+            step("yc", act, T.yo[:, :], T.py[:, 0:128], AF.Copy, deps=["ym"])
+            step("y", dma, "s", T.y[:, :], T.yo[:, :], "out", deps=["yc"])
+
+    for t in range(R):
+        round_steps(t)
+    for word in ORDER.split():
+        key = (word[:-1], int(word[-1]))
+        if key in plan:
+            done[key] = plan.pop(key)()
+    assert not plan
     need("y", ("out", 16 * (1 + 4 + R + 1)))
     need("g", ("loc", local[0]), *[("c" + k, n) for k, n in count.items()])

from concourse.bass import DstId, RemoteDMATransfer
from concourse.mybir import dt, AluOpType, ActivationFunctionType, AxisListType

M, A, E, R = 384, 32, 40, 3
HM = M // 2
SL = 48
SP = 128 + M
QW, QL = 128 + 4 * SL, 128 + 4 * SP
FW = 7500
STEP = 4096.0
CODE, U8, F32, BF, I32, U16 = "float8_e4m3fn_x4", "uint8", "float32", "bfloat16", "int32", "uint16"
ORDER = """
mm00 mm10 sc00 sc10 x10 dq00 dq10 dq20 dq30 c00 c10 fc0 mx0 ba0 bc00 bc10 kt00 kt10 ks00 ks10 lc00 lc10 lc30 lc20 ps0 kf30 kf10 ow0 pc0
bl00 bl10 bl20 bl30 rw0 fl0 mi0 mt30 mt10 mt00 mt20 cs0 ca00 ca10 s10 ca20 ca30 bx0 b00 b10 b30 bw0 b20 ac00 ac10 tc00 nd0 k20 wr0 ac20
eq0 tc10 kf00 kf20 pz0 lg00 lg10 lg20 lg30 gc0 ab20 ab00 ab10 gs0 x20 x30 lw0 pa0 d20 j00 d00 d10 jt0 js0 lm30 lm20 lm00 lm10
ll30 ll20 ll10 ll00 mc0 qc00 qc10 mp0 qs00 qs10
mm01 mm11 sc01 sc11 fc1 x11 dq01 dq11 dq21 dq31 c01 c11 mx1 ba1 bc01 bc11 kt11 kt01 ks11 ks01 lc01 lc31 lc11 lc21 pc1 kf11 kf01 ps1 kf21
pl11 ow1 pl00 bl01 bl11 bl21 bl31 ca01 ca11 kw0 rw1 fl1 mi1 mt01 mt31 mt21 mt11 cs1 s11 ca21 ca31 b21 bw1 b01 bx1 b11 b31 ac01 ac11 nd1 k21
wr1 ac21 eq1 lg31 lg21 lg01 lg11 tc11 kf31 tc01 pz1 gc1 ab01 ab21 ab11 gs1 pl01 x21 x31 pa1 d01 j01 d21 d11 jt1 js1 lm01 lm11 lm21 lm31
ll31 ll21 ll11 ll01 oh1 mc1 qc11 qc01 mp1 pl10 qs01 qs11
mm02 mm12 sc02 sc12 x12 dq02 dq12 dq22 dq32 c02 c12 fc2 ba2 mx2 bc02 bc12 kt12 kt02 ks12 ks02 lc12 lc32 lc22 lc02 pc2 kf12 pl12 kf22 pl02
ps2 xp2 bl02 bl12 bl22 bl32 kf02 ca02 ca22 ow2 ca12 ca32 nd2 x22 x32 rw2 fl2 oh0 mi2 mt32 mt22 mt12 mt02 cs2 s12 b22 b02 tc22 b32 b12 bx2
bw2 tc12 ac02 ac12 tc02 kf32 k22 wr2 lp2 ac22 eq2 pz2 lg12 lg32 lg02 lg22 ab12 ab02 ab22 sg1 pa2 j02 oh2 d12 d02 d22 jt2 js2 lm12 lm02 gx2
sg2 lm32 lm22 w12 sg0 ll32 ll12 ll02 ll22 mc2 mp2 w22 w02 qs02 wi12 oc2 os12 wi22 os22 wi02 os32 os02 qc02 qc12 qs12 ym2 yc2 y2
"""

SCRATCH = {
    "xt": ("sbuf", [128, 512], BF), "xq": ("sbuf", [128, 128], CODE), "xs": ("sbuf", [128, 128], U8),
    "met": ("sbuf", [128, 4 * M], BF),
    "wt": ("sbuf", [128, 512], BF), "wq": ("sbuf", [128, 128], CODE), "ws": ("sbuf", [128, 128], U8),
    "et": ("sbuf", [128, 516], BF), "eq": ("sbuf", [128, 512], CODE), "es": ("sbuf", [128, 512], U8),
    "ints": ("sbuf", [128, 264], I32),
    "cf": ("sbuf", [128, 1100], F32),
    "ff": ("sbuf", [128, FW], F32), "fb": ("sbuf", [128, 1024], BF),
    "kr": ("sbuf", [128, 2, 64], F32),
    "ab": ("sbuf", [128, 3, SL + 32], F32), "jj": ("sbuf", [128, 4, SL + 32], F32), "lm": ("sbuf", [128, 4, 8], F32),
    "offx": ("sbuf", [128, 2], U16),
    "places": ("sbuf", [128, 4], F32), "landp": ("sbuf", [128, 12], F32),
    "yo": ("sbuf", [128, 128], F32),
    "m3": ("sbuf", [128, M], CODE), "ms3": ("sbuf", [128, M], U8),
    "q3": ("sbuf", [128, 128], CODE), "qs3": ("sbuf", [128, 128], U8),
    "pscore": ("psum", [128, 1024], F32), "pblend": ("psum", [128, 2048], F32), "py": ("psum", [128, 512], F32),
}
SEMAPHORES = ["cv", "cs", "ct", "cg", "lx", "lm", "lw", "x0", "xp", "loc", "out"]
for _t in range(R):
    _w = QL if _t == R - 1 else QW
    SCRATCH.update({
        "q%d" % _t: ("sbuf", [128, _w], CODE), "qs%d" % _t: ("sbuf", [128, _w], U8),
        "p%d" % _t: ("sbuf", [128, 128], CODE), "ps%d" % _t: ("sbuf", [128, 128], U8),
        "h%d" % _t: ("sbuf", [128, 512], BF),
        "land%d" % _t: ("sbuf", [128, 16], F32),
        "oc%d" % _t: ("sbuf", [128, 8], U16), "og%d" % _t: ("sbuf", [128, 4], U16),
        "ol%d" % _t: ("sbuf", [128, 32], U16),
    })
    if _t < R - 1:
        SCRATCH.update({"m%d" % _t: ("sbuf", [128, SP], CODE), "ms%d" % _t: ("sbuf", [128, SP], U8)})
    SEMAPHORES += ["x1_%d" % _t, "x2_%d" % _t, "x3_%d" % _t]


def rank_program(g, core, T, topo):
    r = T.rank_of(core)
    if r is None:
        return
    AF, OP, AXIS = ActivationFunctionType, AluOpType, AxisListType.X
    V, S, TE = g.vector, g.scalar, g.tensor
    others = sorted([(r + k) % 4 for k in (1, 2, 3)], key=lambda s: topo.same_plane(topo.chip(core), topo.chip(T.cores[s])))
    queue = {"v": V, "s": S, "t": TE, "g": g, "y": g.sync}
    count = {"v": 0, "s": 0, "t": 0, "g": 0}
    seen = {k: {} for k in queue}
    sem = T.sem

    def need(q, *deps):
        want = {}
        for d in deps:
            if d is not None:
                want[d[0]] = max(want.get(d[0], 0), d[1])
        for n, v in want.items():
            if seen[q].get(n, 0) < v:
                queue[q].wait_ge(sem[n], v)
                seen[q][n] = v

    def did(q, ins):
        count[q] += 1
        ins.then_inc(sem["c" + q], 1)
        return ("c" + q, count[q])

    def ts(out, in0, s1, op0, s2=None, op1=None, deps=()):
        need("v", *deps)
        if op1 is None:
            return did("v", V.tensor_scalar(out, in0, s1, None, op0))
        return did("v", V.tensor_scalar(out, in0, s1, s2, op0, op1))

    def tt(out, a, b, op, deps=()):
        need("v", *deps)
        return did("v", V.tensor_tensor(out, a, b, op))

    def red(out, a, op, deps=()):
        need("v", *deps)
        return did("v", V.tensor_reduce(out, a, AXIS, op))

    def scan(out, a, b, op0, op1, init, deps=()):
        need("v", *deps)
        return did("v", V.tensor_tensor_scan(out, a, b, init, op0, op1))

    def tr(out, a, deps=()):
        need("v", *deps)
        return did("v", V.transpose(out, a))

    def cp(out, a, deps=()):
        need("v", *deps)
        return did("v", V.tensor_copy(out, a))

    def fill(ap, c, deps=()):
        need("v", *deps)
        return did("v", V.memset(ap, c))

    def qmx(o, s, i, deps=()):
        need("v", *deps)
        return did("v", V.quantize_mx(o, s, i))

    def act(out, a, func, deps=(), **k):
        need("s", *deps)
        return did("s", S.activation(out, a, func, **k))

    def mm(out, l, ls, x, xs, start, stop, deps=()):
        need("t", *deps)
        return did("t", TE.matmul_mx(out, l, ls, x, xs, start, stop))

    def io(*a, **k):
        return did("g", g.iota(*a, **k))

    def dma(qn, out, src, sm, deps=()):
        need(qn, *deps)
        queue[qn].dma_start(out, src).then_inc(sem[sm], 16)

    used, cpos = [0], [0]

    def new(n):
        o = used[0]
        used[0] = o + (n + 7) // 8 * 8
        assert used[0] <= FW
        return o

    def F(o, c0, c1, p0=0, p1=128, st=1):
        return T.ff[p0:p1, o + c0:o + c1:st]

    def H(o, c0, c1, p0=0, p1=128):
        return T.fb[p0:p1, o + c0:o + c1]

    def cnew(n):
        o = cpos[0]
        cpos[0] = o + (n + 7) // 8 * 8
        return o

    def C(o, c0, c1, p0=0, p1=128, st=1):
        return T.cf[p0:p1, o + c0:o + c1:st]

    engines = [e for e in topo.engines(core, T.cores[others[0]]) if all(e in topo.engines(core, T.cores[s]) for s in others)]
    ne = len(engines)
    local = [0]

    def send(src, dsts, rsem, deps):
        need("g", *deps)
        ids = []
        for s in others:
            rid, pid, _ = topo.addr(T.cores[s])
            ids.append(DstId(rid=rid, pnc=pid))
        g.remote_dma_fused([RemoteDMATransfer(dst_ids=ids, dma_engine_mask=sum(1 << e for e in engines), remote_sem=sem[rsem],
                                              srcs=[src], dsts=dsts)], local_sem=sem["loc"])
        local[0] += ne

    u8, u32 = dt.uint8, dt.uint32

    dma("y", T.xt[:, 0:4 * A], T.x[:, :], "lx")
    dma("y", T.met[:, :], T.me[:, :], "lm")

    small = {"allow_small_or_imprecise_dtypes": True}
    cNeg, cW, cTO, cZero, cJb, cNm, cRow = [cnew(n) for n in (HM, 128, 64, 32, 32, 32, 32)]
    cM16, cP31, cKb, cOf, cT0, cT1, cNp, cJf, cPb, cFour, c16, cPl = [cnew(n) for n in (1, 1, 3, 1, 1, 1, 3, 1, 2, 4, 3, 3)]
    OH, G, KF, RW3, PA, SG, WO = [new(n) for n in (12, 12, 136, 8 * R, 3, 3, 3)]
    cE, MI, CS, WR, EQ, K2, MR, BW = 0, 128, 192, 384, 512, 640, 768, 896
    i0 = io(T.ints[:, 0:1], [[0, 1]], 0, 1)
    i1 = io(C(c16, 0, 3), [[16, 3]], 0, 0, **small)
    i3 = io(T.ints[:, 8:136], [[1, 128]], 128, -1)
    i2 = io(C(cJb, 0, 32), [[0, 32]], 0, 1, **small)
    i4 = io(C(cRow, 0, 32), [[-2, 32]], 0, 0, **small)
    kPl = io(C(cPl, 0, 3), [[128, 3]], 128, 1, **small)
    i6 = io(C(cFour, 0, 4), [[1, 4]], 1, 0, **small)
    z0 = fill(T.xt[:, 4 * A:512], 0.0)
    z1 = fill(T.et[:, :], 0.0)
    b0 = ts(T.ints[:, 1:2], T.ints[:, 0:1], 15, OP.bitwise_and, deps=[i0])
    b1 = ts(T.ints[:, 2:3], T.ints[:, 0:1], 31, OP.bitwise_and)
    f3 = fill(C(cZero, 0, 32), 0.0)
    a1 = cp(C(cM16, 0, 1), T.ints[:, 1:2], [b0])
    a2 = ts(C(cP31, 0, 1), T.ints[:, 2:3], -2.0, OP.mult, deps=[b1])
    kOx = ts(T.offx[:, 0:2], C(c16, 0, 2), C(cM16, 0, 1), OP.add, deps=[a1, i1])
    qx = qmx(T.xq[:, :], T.xs[:, :], T.xt[:, :], [("lx", 16), z0])
    o0, o1 = A * r, A * r + A
    send(T.xq[:, 0:A].bitcast(u8), [T.q0[:, o0:o1].bitcast(u8)] * 3, "x0", [qx])
    send(T.xs[:, 0:A], [T.qs0[:, o0:o1]] * 3, "x0", [qx])
    i7 = ts(T.et[:, 3:515:4], T.ints[:, 8:136], 128.0, OP.is_equal, 0.5, OP.mult, deps=[i3, z1])
    own = cp(T.q0[:, o0:o1].bitcast(u32), T.xq[:, :].bitcast(u32).indirect(T.offx[:, 0:2]), [kOx, qx])
    owns = act(T.qs0[:, o0:o1], T.xs[:, :].indirect(T.offx[:, 0:2]), AF.Copy, [kOx, qx])
    kNm = act(C(cNm, 0, 32), C(cJb, 0, 32), AF.Copy, [i2], scale=1.0 / 1024, bias=float(HM + 1))
    kJf = act(C(cJf, 0, 1), C(cJb, 0, 1), AF.Copy, scale=1.0 / 1024, bias=1.0)
    for k in range(2):
        kPb = act(C(cPb, k, k + 1), C(cJb, 0, 1), AF.Copy, scale=-1.0 / 1024, bias=M * r - 0.5 - k * 64.0 / 1024)
    kT = act(C(cT0, 0, 1), C(cJb, 0, 1), AF.Copy, scale=-1.0 / 128, bias=(127.0 - SL) / 128)
    kT = act(C(cT1, 0, 1), C(cJb, 0, 1), AF.Copy, scale=-1.0, bias=float(127 - SL + E))
    b3 = ts(T.ints[:, 136:264], T.ints[:, 8:136], 15, OP.bitwise_and)
    for b in range(4):
        ke = qmx(T.eq[:, 128 * b:128 * b + 128], T.es[:, 128 * b:128 * b + 128], T.et[:, 3 - b:515 - b], [i7])
    kW = ts(C(cW, 0, 128), T.ints[:, 136:264], 1.0, OP.min, deps=[b3])
    f0 = fill(C(cNeg, 0, HM), -1e29)
    f2 = fill(H(cE, 0, 128, 0, 32), float(E))
    kKb = ts(C(cKb, 0, 3), C(c16, 0, 3), C(cM16, 0, 1), OP.add, 0.5, OP.add)
    kOf = ts(C(cOf, 0, 1), C(cM16, 0, 1), -15.0, OP.add, STEP, OP.mult)
    fBW = fill(H(BW, 0, 128), 0.0)
    fK2 = fill(H(K2, 96, 104, 0, 32), -64.0)
    fKF = fill(F(KF, 128, 136), 0.0)
    fRW = fill(F(RW3, 0, 8 * R), -1e29)
    f4 = fill(C(cTO, 32, 64), 1.0)
    kTri = ts(C(cTO, 0, 32), C(cRow, 0, 32), C(cP31, 0, 1), OP.is_le, deps=[a2, i4])
    kW = act(C(cW, 0, 128), C(cW, 0, 128), AF.Copy, [kW], scale=1024 * STEP + STEP, bias=-1024 * STEP)
    kNp = act(C(cNp, 0, 3), C(cPl, 0, 3), AF.Copy, [kPl], scale=-1024.0, bias=127.0 * 1024)
    for c in range(3):
        kNp = act(T.ab[:, c, SL:SL + 32], C(cZero, 0, 32), AF.Identity, [f3], bias=C(cPl, c, c + 1))
    consts = [f0, f2, f3, f4, fBW, fK2, fKF, fRW, kKb, kOf, kTri, kW, kNm, kJf, kPb, kT, kNp, i6]
    need("v", *consts)
    need("s", *consts)
    memd = qmx(T.m0[:, 128:SP], T.ms0[:, 128:SP], T.met[:, :], [("lm", 16)])

    plan, done = {}, {}

    def round_steps(t):
        last = t == R - 1
        land = T["land%d" % t]
        q, qs, p, ps, h = T["q%d" % t], T["qs%d" % t], T["p%d" % t], T["ps%d" % t], T["h%d" % t]
        m, ms, b0 = (q, qs, 128 + SP * r) if last else (T["m%d" % t], T["ms%d" % t], 0)
        m0 = b0 + 128
        oc, og, ol = T["oc%d" % t], T["og%d" % t], T["ol%d" % t]
        x1, x2, x3 = "x1_%d" % t, "x2_%d" % t, "x3_%d" % t

        def step(name, fn, *a, **k):
            deps = [(x, t) if isinstance(x, str) else x for x in k.pop("deps")]

            def run():
                assert not any(x in plan for x in deps)
                return fn(*a, deps=[x[:2] if len(x) == 3 else done.get(x) for x in deps], **k)
            plan[(name, t)] = run

        def four(n, k=4):
            return [n + str(a) for a in range(k)]

        if t == 0:
            newq, mem = [own + (0,), owns + (0,), ("x0", 2 * 3 * ne, 0)], [memd + (0,)]
        else:
            newq, mem = [(n, t - 1) for n in ("qc0", "qc1", "qs0", "qs1")], [("mc", t - 1), ("mp", t - 1)]
        RM, JK, C0, C1 = new(M), new(M), new(1), new(1)
        half = [F(RM, k, M, st=2) for k in range(2)]
        top = [F(RM, M - 2 + k, M - 1 + k) for k in range(2)]
        for k in range(2):
            step("mm%d" % k, mm, T.pscore[:, 512 * k:512 * k + HM], q[:, 0:128], qs[:, 0:128], m[:, m0 + HM * k:m0 + HM * k + HM],
                 ms[:, m0 + HM * k:m0 + HM * k + HM], True, True, deps=newq + mem + [("sc%d" % k, t - 1)])
            step("sc%d" % k, scan, half[k], T.pscore[:, 512 * k:512 * k + HM], C(cNeg, 0, HM), OP.max, OP.max, -1e29, deps=["mm%d" % k])
        step("x1", send, F(RM, M - 2, M), [land[:, 4 * r:4 * r + 2]] * 3, x1, deps=["sc0", "sc1"])
        B1, R2, FC, BA, OW = new(64), new(128), new(1), new(1), new(32)
        ME = land[:, 4 * r:4 * r + 1]
        step("c0", act, F(JK, 0, HM), half[0], AF.Sign, scale=-1.0, bias=top[0], accum_out=F(C0, 0, 1), deps=["sc0"])
        step("c1", act, F(JK, HM, M), half[1], AF.Sign, scale=-1.0, bias=top[1], accum_out=F(C1, 0, 1), deps=["sc1"])
        step("fc", ts, F(FC, 0, 1), top[1], top[0], OP.is_gt, 1e5, OP.mult, deps=["sc0", "sc1"])
        step("mx", ts, land[:, 4 * r:4 * r + 2], F(RM, M - 2, M), top[0], OP.max, top[1], OP.max, deps=["sc0", "sc1"])
        step("ba", ts, F(BA, 0, 1), F(C0, 0, 1), F(FC, 0, 1), OP.add, C(cJf, 0, 1), OP.add, deps=["fc", "c0"])
        for k in range(2):
            a, b = 64 * k, 64 * k + 64
            step("bc%d" % k, ts, F(B1, 32 * k, 32 * k + 32, 0, 64), C(cNm, 0, 32, a, b), F(C1, 0, 1, a, b), OP.add, F(BA, 0, 1, a, b), OP.min,
                 deps=["ba", "c1"])
            step("kt%d" % k, tr, T.kr[0:32, :, 32 * k:32 * k + 32], F(B1, 0, 64, 32 * k, 32 * k + 32), deps=["bc0", "bc1"])
            step("ks%d" % k, scan, F(R2, a, b, 0, 32), C(cW, 0, 64, 0, 32), T.kr[0:32, k, :], OP.add, OP.max, 0.0, deps=["kt0", "kt1"])
            step("pl%d" % k, act, T.places[a:b, t:t + 1], F(B1, 32 * k, 32 * k + 1, 0, 64), AF.Identity, bias=C(cPb, k, k + 1, 0, 64),
                 deps=["bc%d" % k])
        for a in range(4):
            step("lc%d" % a, ts, oc[32 * a:32 * a + 32, 0:8], F(R2, 15, 128, 0, 32, 16), C(cOf, 0, 1, 0, 32), OP.add, -1.0, OP.add,
                 deps=["ks0", "ks1"])
            step("kf%d" % a, act, F(KF, 0, 128, 32 * a, 32 * a + 32), T.kr[0:32, :, :], AF.Copy, deps=["kt0", "kt1"])
            bank = T.pblend[:, 512 * a:512 * a + 128]
            e, es = T.eq[:, 128 * a:128 * a + 128], T.es[:, 128 * a:128 * a + 128]
            step("dq%d" % a, mm, bank, e, es, q[:, 0:128], qs[:, 0:128], True, False, deps=newq + [ke + (0,), ("ca%d" % a, t - 1)])
            step("bl%d" % a, mm, bank, e, es, p[:, :], ps[:, :], False, True, deps=["pc", "ps"])
            if last and a % 2:
                step("ca%d" % a, cp, h[:, a:512:4], bank, deps=["bl%d" % a])
            else:
                step("ca%d" % a, act, h[:, a:512:4], bank, AF.Copy, deps=["bl%d" % a])
        step("ow", act, F(OW, 0, 32), C(cZero, 0, 32), AF.Identity, bias=ME, deps=["mx"])
        step("pc", cp, p[:, :].bitcast(u32), m[:, m0:m0 + M].bitcast(u32).indirect(oc[:, 0:8]), deps=four("lc") + mem)
        step("ps", act, ps[:, :], ms[:, m0:m0 + M].indirect(oc[:, 0:8]), AF.Copy, deps=four("lc") + mem)
        step("nd", qmx, m[:, b0:m0], ms[:, b0:m0], h[:, :], deps=four("ca"))
        FL, AC, S1, TC, T1, PS, P = new(1), new(3), new(1), new(1), new(1), new(1), new(1)
        RW = RW3 + 8 * t
        got = (x1, 3 * ne, 0)
        step("rw", scan, F(RW, 1, 5), land[:, 0:16:4], land[:, 1:16:4], OP.max, OP.max, -1e29, deps=[got, "mx"])
        if r == 1:
            step("fl", ts, F(FL, 0, 1), land[:, 0:1], land[:, 1:2], OP.max, ME, OP.is_lt, deps=[got, "mx"])
        if r == 2:
            step("fl", ts, F(FL, 0, 1), land[:, 12:13], land[:, 13:14], OP.max, ME, OP.is_le, deps=[got, "mx"])
        c, op = ((4, OP.is_ge), (4, OP.is_ge), (2, OP.is_gt), (3, OP.is_gt))[r]
        step("mi", ts, H(MI, 0, 32), F(OW, 0, 32), F(RW, c, c + 1), op, *((F(FL, 0, 1), OP.mult) if r in (1, 2) else ()), deps=["rw", "fl", "ow"])
        for a in range(4):
            step("mt%d" % a, tr, H(MR, 32 * a, 32 * a + 32, 0, 32), H(MI, 0, 32, 32 * a, 32 * a + 32), deps=["mi"])
            step("lg%d" % a, ts, og[32 * a:32 * a + 32, 0:3], F(AC, 0, 3, 0, 32), 0.5, OP.mult, 64.0, OP.add, deps=four("ac", 3))
        step("cs", scan, H(CS, 0, 128, 0, 32), H(MR, 0, 128, 0, 32), H(cE, 0, 128, 0, 32), OP.add, OP.min, 0.0, deps=four("mt"))
        for c in range(2):
            step("ac%d" % c, act, F(new(128), 0, 128, 0, 32), H(CS, 0, 128, 0, 32), AF.Sign, scale=-1.0, bias=C(cKb, c, c + 1, 0, 32),
                 accum_out=F(AC, c, c + 1, 0, 32), deps=["cs"])
        step("k2", ts, H(K2, 0, 96, 0, 32), H(CS, 32, 128, 0, 32), C(cKb, 2, 3, 0, 32), OP.is_le, 2.0, OP.mult, deps=["cs"])
        step("ac2", red, F(AC, 2, 3, 0, 32), H(K2, 0, 97, 0, 32), OP.add, deps=["k2"])
        if last:
            step("x2", send, m[:, b0:m0].bitcast(u8), [m[:, b0:m0].bitcast(u8)] * 3, x2, deps=["nd"])
            step("x3", send, ms[:, b0:m0], [ms[:, b0:m0]] * 3, x3, deps=["nd"])
        else:
            k0 = 128 + SL * r
            step("gc", cp, q[:, k0:k0 + SL].bitcast(u32), m[:, :].bitcast(u32).indirect(og[:, 0:3]), deps=four("lg") + ["nd"])
            step("gs", act, qs[:, k0:k0 + SL], ms[:, :].indirect(og[:, 0:3]), AF.Copy, deps=four("lg") + ["nd"])
            step("x2", send, q[:, k0:k0 + E].bitcast(u8), [q[:, k0:k0 + E].bitcast(u8)] * 3, x2, deps=["gc"])
            step("x3", send, qs[:, k0:k0 + E], [qs[:, k0:k0 + E]] * 3, x3, deps=["gs"])
        JT, JS = new(128), new(128)
        step("s1", act, F(new(4), 0, 4), F(RW, 0, 4), AF.Sign, scale=-1.0, bias=F(RW, 4, 5), accum_out=F(S1, 0, 1), deps=["rw"])
        step("tc0", act, F(TC, 0, 1), F(S1, 0, 1), AF.Identity, scale=SL / 128.0, bias=C(cT0, 0, 1), deps=["s1"])
        step("tc1", act, F(T1, 0, 1), F(S1, 0, 1), AF.Identity, scale=float(SL), bias=C(cT1, 0, 1), deps=["s1"])
        if last:
            step("tc2", act, F(PS, 0, 1), F(S1, 0, 1), AF.Copy, scale=float(SP), bias=float(128 - SP), deps=["s1"])
        step("bw", act, H(BW, 0, 32), C(cTO, 0, 32), AF.Identity, scale=F(S1, 0, 1), deps=["s1"])
        step("bx", act, H(BW, 32, 64, 64, 128), C(cTO, 32, 64, 0, 64), AF.Identity, scale=F(S1, 0, 1, 0, 64), deps=["s1"])
        for k, (a, b, c) in enumerate(((0, 1, 1), (1, 2, 2), (0, 3, 2), (2, 3, 3))):
            step("b%d" % k, act, H(BW, 32 * c, 32 * c + 32, 32 * b, 32 * b + 32), C(cTO, 32, 64, 32 * a, 32 * a + 32), AF.Identity,
                 scale=F(S1, 0, 1, 32 * a, 32 * a + 32), deps=["s1"])
        step("wr", tr, H(WR, 0, 128), H(BW, 0, 128), deps=["bw", "bx"] + four("b"))
        step("eq", ts, H(EQ, 0, 128), H(WR, 0, 128), F(S1, 0, 1), OP.is_equal, deps=["wr"])
        step("pz", act, F(new(128), 0, 128), H(EQ, 0, 128), AF.Identity, bias=F(TC, 0, 1), accum_out=F(P, 0, 1), deps=["eq", "tc0"])
        step("pa", ts, F(PA, t, t + 1), F(P, 0, 1), F(T1, 0, 1), OP.is_le, F(PS if last else P, 0, 1), OP.mult, deps=["pz", "tc1", "tc2"])
        step("j0", ts, T.jj[:, 0, SL:SL + 32], C(cJb, 0, 32), F(PA, t, t + 1), OP.add, deps=["pa"])
        for c in range(3):
            step("ab%d" % c, act, T.ab[:, c, 0:SL], F(KF, 0, 136).indirect(og[:, 0:3]), AF.Abs, scale=1024.0, bias=C(cNp, c, c + 1),
                 deps=four("lg") + four("kf"))
            step("d%d" % c, scan, T.jj[:, c + 1, :], T.ab[:, c, :], T.ab[:, c, :], OP.min, OP.min, 1e9, deps=["ab%d" % c])
        step("jt", tr, F(JT, 0, 128), T.jj[:, :, SL:SL + 32], deps=["j0"] + four("d", 3))
        step("js", scan, F(JS, 0, 128), C(cW, 0, 128), F(JT, 0, 128), OP.add, OP.max, 0.0, deps=["jt"])
        for a in range(4):
            out, src = T.lm[0:32, :, 2 * a:2 * a + 2], F(JS, 15, 128, 32 * a, 32 * a + 32, 16)
            if a < 2:
                step("lm%d" % a, cp, out, src, deps=["js"])
            else:
                step("lm%d" % a, act, out, src, AF.Copy, deps=["js"])
            step("ll%d" % a, ts, ol[32 * a:32 * a + 32, :], T.lm[0:32, :, :], C(cOf, 0, 1, 0, 32), OP.add, deps=four("lm"))
        if t == R - 2:
            m2, ms2, c0 = T["q%d" % (t + 1)], T["qs%d" % (t + 1)], 256 + SP * r
        elif last:
            m2, ms2, c0 = T.m3, T.ms3, 0
        else:
            m2, ms2, c0 = T["m%d" % (t + 1)], T["ms%d" % (t + 1)], 128
        d = four("ll") + ["nd"] + mem
        step("mc", cp, m2[:, c0:c0 + M].bitcast(u32), m[:, b0:b0 + SP].bitcast(u32).indirect(ol[:, 8:32]), deps=d)
        step("mp", act, ms2[:, c0:c0 + M], ms[:, b0:b0 + SP].indirect(ol[:, 8:32]), AF.Copy, deps=d)
        q2, qs2 = T["q%d" % (t + 1)], T["qs%d" % (t + 1)]
        d = four("ll") + newq + ["nd", "gc", "gs"]
        for k in range(2):
            step("qc%d" % k, cp, q2[:, 64 * k:64 * k + 64].bitcast(u32), q[:, :].bitcast(u32).indirect(ol[:, 4 * k:4 * k + 4]),
                 deps=d + [(x2, 3 * ne, 0)])
        step("qs0", act, qs2[:, 0:64], qs[:, :].indirect(ol[:, 0:4]), AF.Copy, deps=d + [(x3, 3 * ne, 0)])
        step("qs1", cp, qs2[:, 64:128], qs[:, :].indirect(ol[:, 4:8]), deps=d + [(x3, 3 * ne, 0)])
        step("oh", ts, F(OH, t, 12, st=3), C(cFour, 0, 4), F(S1, 0, 1), OP.is_equal, deps=["s1"])
        step("sg", act, F(SG, t, t + 1), F(PA, t, t + 1), AF.Sign, bias=-0.5, deps=["pa"])
        if t == 0:
            step("lw", dma, "y", T.wt[:, :], T.w[:, :], "lw", deps=[got])
            step("kw", qmx, T.wq[:, :], T.ws[:, :], T.wt[:, :], deps=[("lw", 16, 0)])
        if last:
            pl = [(n, c) for c in range(R) for n in ("pl0", "pl1")]
            step("xp", send, T.places[:, 0:R], [T.landp[:, R * r:R * r + R]] * 3, "xp", deps=pl)
            step("lp", cp, T.landp[:, R * r:R * r + R], T.places[:, 0:R], deps=pl + [("xp", 3 * ne, 0)])
            step("gx", tt, F(G, 0, 12), F(OH, 0, 12), T.landp[:, 0:12], OP.mult, deps=[("oh", c) for c in range(R)] + ["lp"])
            for c in range(R):
                step("w%d" % c, act, F(new(4), 0, 4), F(G, c, 12, st=3), AF.Identity, scale=F(SG, c, c + 1), bias=-0.125,
                     accum_out=F(WO, c, c + 1), deps=[("sg", c), "gx"])
                step("wi%d" % c, dma, "y", T.wi[c:c + 1, :], F(WO, c, c + 1), "out", deps=["w%d" % c])
            step("oc", dma, "y", T.oc[:, :], T.m3[:, :].bitcast(u8), "out", deps=["mc"])
            for k in range(4):
                step("os%d" % k, dma, "y", T.osc[4 * k:4 * k + 4, :], T.ms3[32 * k:32 * k + 4, :], "out", deps=["mp"])
            step("ym", mm, T.py[:, 0:128], T.wq[:, :], T.ws[:, :], T.q3[:, :], T.qs3[:, :], True, True, deps=[("kw", 0), "qc0", "qc1", "qs0", "qs1"])
            step("yc", act, T.yo[:, :], T.py[:, 0:128], AF.Copy, deps=["ym"])
            step("y", dma, "s", T.y[:, :], T.yo[:, :], "out", deps=["yc"])

    for t in range(R):
        round_steps(t)
    for word in ORDER.split():
        key = (word[:-1], int(word[-1]))
        if key in plan:
            done[key] = plan.pop(key)()
    assert not plan
    need("y", ("out", 16 * (1 + 4 + R + 1)))
    need("g", ("loc", local[0]), *[("c" + k, n) for k, n in count.items()])
